import numpy as np
import ml_dtypes


def mxq(x, axis, fmt="e4m3"):
    dtype, down = {"e4m3": (ml_dtypes.float8_e4m3fn, 7), "e5m2": (ml_dtypes.float8_e5m2, 14)}[fmt]
    v = np.moveaxis(np.asarray(x, np.float32).astype(ml_dtypes.bfloat16).astype(np.float64), axis, -1)
    blocks = v.reshape(v.shape[:-1] + (-1, 32))
    amax = np.abs(blocks).max(-1, keepdims=True)
    byte = np.maximum(np.where(amax > 0, np.frexp(amax)[1] - 1 + 127, 0) - down, 1)
    scale = np.exp2(byte - 127.0)
    codes = (blocks / scale).astype(np.float32).astype(dtype).astype(np.float64)
    return np.moveaxis((codes * scale).reshape(v.shape), -1, axis)


WIDE = False


def mx_kscale(k):
    if not WIDE:
        return np.ones(k)
    levels = np.array([10, -10, 5, -5, 0])
    if k % 512:
        return np.exp2(np.random.permutation(np.resize(levels, k // 32))).repeat(32)
    a = np.empty((k // 512, 16))
    for p in range(k // 512):
        a[p, :8] = np.random.permutation(np.resize(levels, 8))
        for g in range(8):
            far = levels[np.abs(levels - a[p, g]) >= 10]
            a[p, g + 8] = far[np.random.randint(len(far))]
    return np.exp2(a.ravel()).repeat(32)


BF16 = ml_dtypes.bfloat16


def bf(x):
    return np.asarray(x, np.float32).astype(BF16)


def f64(x):
    return np.asarray(x).astype(np.float64)


E2M1 = np.array([0.0, 0.5, 1.0, 1.5, 2.0, 3.0, 4.0, 6.0, -0.0, -0.5, -1.0, -1.5, -2.0, -3.0, -4.0, -6.0])


def pack_weight(w, fmt):
    k, n = w.shape
    w = f64(bf(w)).reshape(k // 32, 32, n)
    amax = np.abs(w).max(1)
    if fmt == "e4m3":
        byte = np.frexp(amax)[1] - 1 + 127 - 7
    else:
        mant, ex = np.frexp(amax / 6.0)
        byte = np.where(mant > 0.5, ex, ex - 1) + 127
    byte = np.clip(np.where(amax > 0, byte, 1), 1, 254)
    scaled = (w * np.exp2(127.0 - byte)[:, None, :]).reshape(k, n).astype(np.float32)
    by_word = np.ascontiguousarray(scaled.reshape(k // 512, 128, 4, n).transpose(0, 1, 3, 2))
    if fmt == "e4m3":
        words = by_word.astype(ml_dtypes.float8_e4m3fn).view(np.uint8)
    else:
        c = by_word.astype(ml_dtypes.float4_e2m1fn).view(np.uint8) & 0xF
        words = c[..., 0::2] | (c[..., 1::2] << 4)
    return np.ascontiguousarray(words), np.ascontiguousarray(byte.astype(np.uint8).reshape(k // 512, 16, n))


def unpack_weight(words, scales, fmt):
    g, p, n, _ = words.shape
    if fmt == "e4m3":
        vals = np.ascontiguousarray(words).view(ml_dtypes.float8_e4m3fn).astype(np.float64)
    else:
        nib = np.empty((g, p, n, 4), np.uint8)
        nib[..., 0::2] = words & 0xF
        nib[..., 1::2] = words >> 4
        vals = E2M1[nib]
    vals = vals * np.repeat(np.exp2(scales.astype(np.float64) - 127.0), 8, axis=1)[..., None]
    return vals.transpose(0, 1, 3, 2).reshape(g * 512, n)
def pack4(w):
    words, scales = pack_weight(w, "e2m1")
    return words.reshape(words.shape[0], 128, -1), scales


def unpack4(words, scales):
    return unpack_weight(words.reshape(words.shape[0], 128, -1, 2), scales, "e2m1")


def planes(Y):
    n, m = Y.shape
    b = f64(bf(Y)).reshape(n // 32, 32, m)
    amax = np.abs(b).max(1)
    byte = np.clip(np.where(amax > 0, np.frexp(amax)[1] - 1 + 127 - 7, 1), 1, 254)
    codes = (b * np.exp2(127.0 - byte)[:, None, :]).reshape(n, m).astype(np.float32).astype(ml_dtypes.float8_e4m3fn).view(np.uint8)
    words = codes.reshape(n // 512, 128, 4, m).transpose(0, 1, 3, 2)
    return np.ascontiguousarray(words), np.ascontiguousarray(byte.astype(np.uint8).reshape(n // 512, 16, m))


M, D, F = 768, 1024, 2048


def setup_inputs():
    s = mx_kscale(D)
    t = mx_kscale(F)
    z = np.random.randn(M, D)
    gain = np.exp(0.7 * np.random.randn(D))
    p = np.random.randn(D, F) / np.sqrt(F)
    p = p / s[:, None] * t[None, :]
    p_words, p_scales = pack4(p)
    r_words, r_scales = pack4(p.T)
    return {
        "x": bf(z * gain * s),
        "p_words": p_words,
        "p_scales": p_scales,
        "h": bf(np.random.randn(M, F) * t),
        "lam": bf(np.exp(0.3 * np.random.randn(F)) / t**2),
        "r_words": r_words,
        "r_scales": r_scales,
        "gamma": bf(gain * s),
    }


def reference(x, p_words, p_scales, h, lam, r_words, r_scales, gamma):
    P = unpack4(p_words, p_scales)
    R = unpack4(r_words, r_scales)
    E = ((mxq(f64(x), 1, "e4m3") @ P) - f64(h)) * f64(lam)
    y = (mxq(E, 1, "e4m3") @ R) * f64(gamma)
    Y = y.T
    words, scales = planes(Y)
    return y, words, scales

@@ -1,0 +1,541 @@
+from contextlib import ExitStack
+
+import concourse.mybir as mybir
+from concourse.masks import make_identity
+
+M, D, F = 768, 1024, 2048
+FLOPS = 2 * 2 * M * D * F
+
+F32 = mybir.dt.float32
+BF16 = mybir.dt.bfloat16
+I32 = mybir.dt.int32
+U32 = mybir.dt.uint32
+U8 = mybir.dt.uint8
+FP8X4 = mybir.dt.float8_e4m3fn_x4
+FP4X4 = mybir.dt.float4_e2m1fn_x4
+SUB = mybir.AluOpType.subtract
+MULT = mybir.AluOpType.mult
+
+P = 128
+K = 512
+TILES = M // P
+GD = D // K
+GF = F // K
+
+
+def tile_feature_distillation_gradient_h1_kernel(
+    tc, x, p_words, p_scales, h, lam, r_words, r_scales, gamma, out_0, out_1, out_2
+):
+    nc = tc.nc
+    with ExitStack() as ctx:
+        keep = ctx.enter_context(tc.tile_pool(name="keep", bufs=1))
+        work = ctx.enter_context(tc.tile_pool(name="work", bufs=4))
+        sums = ctx.enter_context(tc.psum_pool(name="sums", bufs=4))
+        turns = ctx.enter_context(tc.psum_pool(name="turns", bufs=3))
+        fixed = ctx.enter_context(tc.psum_pool(name="fixed", bufs=1))
+        ctx.enter_context(tc.manual_schedule())
+
+        def kept(name, shape, dtype):
+            return keep.tile(shape, dtype, name=name, align_bytes=64)
+
+        ident = kept("ident", [P, P], F32)
+        x_sb = [kept("x%d" % i, [P, D], BF16) for i in range(TILES)]
+        h_sb = [kept("h%d" % i, [P, F], BF16) for i in range(TILES)]
+        p_codes = kept("p_codes", [P, GD, 2 * F], U8)
+        p_plane = kept("p_plane", [P, GD, F], U8)
+        r_codes = kept("r_codes", [P, GF, 2 * D], U8)
+        r_plane = kept("r_plane", [P, GF, D], U8)
+        lam_rows = kept("lam_rows", [P, GF, 4], BF16)
+        gamma_rows = kept("gamma_rows", [P, 8], BF16)
+        lam_all = kept("lam_all", [P, F], BF16)
+        gamma_all = kept("gamma_all", [P, D], BF16)
+        x_codes = [kept("x_codes%d" % i, [P, GD * P], U32) for i in range(TILES)]
+        x_plane = [kept("x_plane%d" % i, [P, GD * P], U8) for i in range(TILES)]
+        e_codes = [kept("e_codes%d" % i, [P, GF * P], U32) for i in range(TILES)]
+        e_plane = [kept("e_plane%d" % i, [P, GF * P], U8) for i in range(TILES)]
+        e_bf = [kept("e_bf%d" % i, [P, F], BF16) for i in range(TILES)]
+        y_f32 = [kept("y_f32_%d" % i, [P, D], F32) for i in range(TILES)]
+        y_bf = [kept("y_bf%d" % i, [P, D], BF16) for i in range(TILES)]
+        y_codes = kept("y_codes", [P, GD, M], U32)
+        y_plane = kept("y_plane", [P, GD, M], U8)
+
+        lam_bank = fixed.tile([P, 4 * P], F32, name="lam_bank")
+        held = {}
+
+        def rows(i):
+            return slice(i * P, (i + 1) * P)
+
+        def cols(c, width=K):
+            return slice(c * width, (c + 1) * width)
+
+        def by_word_half(ap):
+            return ap.rearrange("m (p u e) -> m u p e", u=2, e=2)
+
+        def as_word_half(ap):
+            return ap.rearrange("m (u p e) -> m u p e", u=2, e=2)
+
+        def zero_plane(plane, part):
+            nc.vector.memset(plane[:, :, part].bitcast(I32), 0)
+
+        def load_plane(plane, scales, part, r):
+            nc.sync.dma_start(
+                out=plane[r:P:32, :, part].bitcast(I32),
+                in_=scales[:, r:16:4, part].rearrange("g q n -> q g n").bitcast(I32),
+            )
+
+        def load_codes(codes, words, part):
+            nc.sync.dma_start(
+                out=codes[:, :, part].bitcast(I32),
+                in_=words[:, :, part].rearrange("g p n -> p g n").bitcast(I32),
+            )
+
+        def load_x(i):
+            nc.sync.dma_start(out=x_sb[i][:], in_=x[rows(i), :])
+
+        def load_h(i, part=slice(0, F)):
+            nc.sync.dma_start(out=h_sb[i][:, part], in_=h[rows(i), part])
+
+        def load_vectors():
+            nc.gpsimd.dma_start(out=lam_rows[:], in_=lam.rearrange("(c p t) -> p c t", p=P, t=4))
+            nc.gpsimd.dma_start(out=gamma_rows[:], in_=gamma.rearrange("(p t) -> p t", p=P))
+
+        def turn(key, sources, bank=None):
+            if bank is None:
+                bank = turns.tile([P, 4 * P], F32, name="turn_bank")
+            for j, source in enumerate(sources):
+                nc.tensor.transpose(bank[:, cols(j, P)], source, ident[:])
+            held[key] = bank
+
+        def gather(key, groups):
+            bank = held.pop(key)
+            grouped = work.tile([P, 2 * K], BF16, name="grouped", align_bytes=64, bufs=6)
+            nc.scalar.copy(
+                out=grouped[:, : groups * K].bitcast(F32).rearrange("p (g m u) -> p g m u", g=groups, u=2),
+                in_=bank[:, : groups * 2 * P].rearrange("p (g u m) -> p g m u", g=groups, u=2),
+            )
+            held[key + ("grouped",)] = grouped
+
+        def tc_lam(half):
+            words = lam_rows[:].rearrange("p c t -> p (c t)").bitcast(F32)
+            turn(("lam", half), [words[:, j : j + 1].to_broadcast([P, P]) for j in range(4 * half, 4 * half + 4)], lam_bank if half == 1 else None)
+
+        def cc_lam(half):
+            nc.scalar.copy(out=lam_all[:, cols(half, 2 * K)].bitcast(F32), in_=held.pop(("lam", half))[:])
+
+        def tc_gamma():
+            words = gamma_rows[:].bitcast(F32)
+            turn(("gamma",), [words[:, j : j + 1].to_broadcast([P, P]) for j in range(4)])
+
+        def cc_gamma():
+            nc.scalar.copy(
+                out=gamma_all[:].bitcast(F32).rearrange("q (p j) -> q p j", j=4),
+                in_=held.pop(("gamma",))[:].rearrange("q (j p) -> q p j", j=4),
+            )
+
+        def tx(i):
+            words = x_sb[i][:].bitcast(F32)
+            turn(("x", i), [words[:, 256 * g + u : 256 * (g + 1) : 2] for g in range(GD) for u in range(2)])
+
+        def txg(i, g):
+            words = x_sb[i][:].bitcast(F32)
+            turn(("x", i, g), [words[:, 256 * g + u : 256 * (g + 1) : 2] for u in range(2)])
+
+        def cxg(i, g):
+            gather(("x", i, g), 1)
+
+        def qxg(i, g):
+            nc.vector.quantize_mx(
+                out=x_codes[i][:, cols(g, P)].bitcast(FP8X4),
+                scales=x_plane[i][:, cols(g, P)],
+                in_=held.pop(("x", i, g, "grouped"))[:, :K],
+            )
+
+        def cx(i):
+            gather(("x", i), 2)
+
+        def qx(i):
+            nc.vector.quantize_mx(
+                out=x_codes[i][:].bitcast(FP8X4), scales=x_plane[i][:], in_=held.pop(("x", i, "grouped"))[:]
+            )
+
+        def m1(i, c):
+            bank = sums.tile([P, K], F32, name="sum_bank")
+            for g in range(GD):
+                nc.tensor.matmul_mx(
+                    out=bank[:],
+                    lhsT=x_codes[i][:, cols(g, P)].bitcast(FP8X4),
+                    lhsT_scale=x_plane[i][:, cols(g, P)],
+                    rhs=p_codes[:, g, cols(c, 2 * K)].bitcast(FP4X4),
+                    rhs_scale=p_plane[:, g, cols(c)],
+                    start=(g == 0),
+                    stop=(g == GD - 1),
+                )
+            held[("s1", i, c)] = bank
+
+        def sub(i, c):
+            diff = work.tile([P, K], F32, name="diff", align_bytes=64, bufs=8)
+            nc.vector.tensor_tensor(
+                out=as_word_half(diff[:]),
+                in0=by_word_half(held.pop(("s1", i, c))[:]),
+                in1=by_word_half(h_sb[i][:, cols(c)]),
+                op=SUB,
+            )
+            held[("diff", i, c)] = diff
+
+        def mul(engine, i, c):
+            engine.tensor_tensor(
+                out=e_bf[i][:, cols(c)], in0=held.pop(("diff", i, c))[:], in1=lam_all[:, cols(c)], op=MULT
+            )
+
+        def gmul(i, c):
+            mul(nc.gpsimd, i, c)
+
+        def vmul(i, c):
+            mul(nc.vector, i, c)
+
+        def vmulp(i, c):
+            nc.vector.tensor_tensor(
+                out=e_bf[i][:, cols(c)],
+                in0=held.pop(("diff", i, c))[:],
+                in1=lam_bank[:].bitcast(BF16)[:, cols(c - 2)],
+                op=MULT,
+            )
+
+        def te(i, half):
+            words = e_bf[i][:].bitcast(F32)
+            turn(("e", i, half), [words[:, cols(j, P)] for j in range(4 * half, 4 * half + 4)])
+
+        def ce(i, half):
+            gather(("e", i, half), 2)
+
+        def qe(i, half):
+            nc.vector.quantize_mx(
+                out=e_codes[i][:, cols(half, 2 * P)].bitcast(FP8X4),
+                scales=e_plane[i][:, cols(half, 2 * P)],
+                in_=held.pop(("e", i, half, "grouped"))[:],
+            )
+
+        def m2(i, d):
+            bank = sums.tile([P, K], F32, name="sum_bank")
+            for g in range(GF):
+                nc.tensor.matmul_mx(
+                    out=bank[:],
+                    lhsT=e_codes[i][:, cols(g, P)].bitcast(FP8X4),
+                    lhsT_scale=e_plane[i][:, cols(g, P)],
+                    rhs=r_codes[:, g, cols(d, 2 * K)].bitcast(FP4X4),
+                    rhs_scale=r_plane[:, g, cols(d)],
+                    start=(g == 0),
+                    stop=(g == GF - 1),
+                )
+            held[("s2", i, d)] = bank
+
+        def gam(i, d):
+            nc.vector.tensor_tensor(
+                out=y_f32[i][:, cols(d)], in0=held.pop(("s2", i, d))[:], in1=gamma_all[:, cols(d)], op=MULT
+            )
+
+        def gamb(i, d):
+            nc.vector.tensor_tensor(
+                out=as_word_half(y_bf[i][:, cols(d)]),
+                in0=by_word_half(held[("s2", i, d)][:]),
+                in1=by_word_half(gamma_all[:, cols(d)]),
+                op=MULT,
+            )
+
+        def cast(i, d):
+            nc.scalar.copy(out=as_word_half(y_bf[i][:, cols(d)]), in_=by_word_half(y_f32[i][:, cols(d)]))
+
+        def store_y(i, d):
+            nc.sync.dma_start(out=out_0[rows(i), cols(d)], in_=y_f32[i][:, cols(d)])
+
+        def ty(i, ds):
+            words = y_bf[i][:].bitcast(F32)
+            turn(("y", i, ds), [words[:, cols(2 * d + u, P)] for d in ds for u in range(2)])
+
+        def cy(i, ds):
+            gather(("y", i, ds), len(ds))
+            grouped = held.pop(("y", i, ds, "grouped"))
+            for j, d in enumerate(ds):
+                held[("yg", i, d)] = grouped[:, cols(j)]
+
+        def qy(i, d):
+            nc.vector.quantize_mx(
+                out=y_codes[:, d, rows(i)].bitcast(FP8X4), scales=y_plane[:, d, rows(i)], in_=held.pop(("yg", i, d))
+            )
+
+        def store_codes(i, part=slice(0, GD)):
+            nc.sync.dma_start(
+                out=out_1.rearrange("g p m t -> p g (m t)")[:, part, cols(i, 4 * P)].bitcast(I32),
+                in_=y_codes[:, part, rows(i)].bitcast(I32),
+            )
+
+        def store_plane(r, engine):
+            engine.dma_start(
+                out=out_2[:, r:16:4, :].rearrange("g q m -> q g m").bitcast(I32),
+                in_=y_plane[r:P:32, :, :].bitcast(I32),
+            )
+
+        zero_plane(p_plane, cols(0, 2 * K))
+        zero_plane(p_plane, cols(1, 2 * K))
+        zero_plane(r_plane, cols(0))
+        zero_plane(r_plane, cols(1))
+        make_identity(nc, ident[:])
+        load_x(0)
+        load_vectors()
+        load_x(1)
+        load_plane(p_plane, p_scales, cols(0, 2 * K), 0)
+        load_plane(p_plane, p_scales, cols(0, 2 * K), 1)
+        load_plane(p_plane, p_scales, cols(0, 2 * K), 2)
+        load_plane(p_plane, p_scales, cols(0, 2 * K), 3)
+        load_codes(p_codes, p_words, cols(0, 2 * K))
+        load_h(0, cols(0, 2 * K))
+        load_codes(p_codes, p_words, cols(1, 2 * K))
+        load_h(1, cols(0, 2 * K))
+        load_plane(p_plane, p_scales, cols(1, 2 * K), 0)
+        load_plane(p_plane, p_scales, cols(1, 2 * K), 1)
+        load_plane(p_plane, p_scales, cols(1, 2 * K), 2)
+        load_plane(p_plane, p_scales, cols(1, 2 * K), 3)
+        load_codes(p_codes, p_words, cols(2, 2 * K))
+        load_h(0, cols(1, 2 * K))
+        load_x(2)
+        load_codes(p_codes, p_words, cols(3, 2 * K))
+        load_h(1, cols(1, 2 * K))
+        load_h(2, cols(0, 2 * K))
+        load_x(3)
+        load_h(2, cols(1, 2 * K))
+        load_plane(r_plane, r_scales, cols(0), 0)
+        load_plane(r_plane, r_scales, cols(0), 1)
+        load_plane(r_plane, r_scales, cols(0), 2)
+        load_plane(r_plane, r_scales, cols(0), 3)
+        load_plane(r_plane, r_scales, cols(1), 0)
+        load_plane(r_plane, r_scales, cols(1), 1)
+        load_plane(r_plane, r_scales, cols(1), 2)
+        load_plane(r_plane, r_scales, cols(1), 3)
+        load_codes(r_codes, r_words, cols(0, 2 * K))
+        load_codes(r_codes, r_words, cols(1, 2 * K))
+        load_x(4)
+        load_h(3)
+        load_x(5)
+        load_h(4)
+        load_h(5)
+        txg(0, 0)
+        cxg(0, 0)
+        qxg(0, 0)
+        txg(0, 1)
+        cxg(0, 1)
+        qxg(0, 1)
+        tx(1)
+        cx(1)
+        tc_lam(0)
+        cc_lam(0)
+        m1(0, 0)
+        qx(1)
+        m1(1, 0)
+        tc_lam(1)
+        cc_lam(1)
+        m1(0, 1)
+        m1(1, 1)
+        sub(0, 0)
+        gmul(0, 0)
+        sub(1, 0)
+        gmul(1, 0)
+        m1(0, 2)
+        sub(0, 1)
+        gmul(0, 1)
+        m1(1, 2)
+        sub(1, 1)
+        tx(2)
+        cx(2)
+        m1(0, 3)
+        sub(0, 2)
+        m1(1, 3)
+        sub(1, 2)
+        vmulp(0, 2)
+        qx(2)
+        gmul(1, 1)
+        sub(0, 3)
+        vmulp(1, 2)
+        sub(1, 3)
+        gmul(1, 3)
+        vmulp(0, 3)
+        m1(2, 0)
+        m1(2, 1)
+        tx(3)
+        cx(3)
+        te(0, 0)
+        ce(0, 0)
+        te(0, 1)
+        ce(0, 1)
+        tc_gamma()
+        cc_gamma()
+        sub(2, 0)
+        sub(2, 1)
+        m1(2, 2)
+        m1(2, 3)
+        qx(3)
+        qe(0, 0)
+        qe(0, 1)
+        gmul(2, 0)
+        gmul(2, 1)
+        sub(2, 2)
+        sub(2, 3)
+        gmul(2, 3)
+        vmulp(2, 2)
+        m2(0, 0)
+        m2(0, 1)
+        te(1, 0)
+        ce(1, 0)
+        te(1, 1)
+        ce(1, 1)
+        tx(4)
+        cx(4)
+        gam(0, 0)
+        store_y(0, 0)
+        cast(0, 0)
+        gam(0, 1)
+        store_y(0, 1)
+        cast(0, 1)
+        qe(1, 0)
+        qe(1, 1)
+        qx(4)
+        m1(3, 0)
+        m1(3, 1)
+        sub(3, 0)
+        gmul(3, 0)
+        m2(1, 0)
+        sub(3, 1)
+        gmul(3, 1)
+        m1(3, 2)
+        gam(1, 0)
+        store_y(1, 0)
+        cast(1, 0)
+        m1(3, 3)
+        sub(3, 2)
+        m2(1, 1)
+        sub(3, 3)
+        gmul(3, 3)
+        vmulp(3, 2)
+        gam(1, 1)
+        store_y(1, 1)
+        te(2, 0)
+        ce(2, 0)
+        te(2, 1)
+        ce(2, 1)
+        ty(0, (0, 1))
+        cy(0, (0, 1))
+        tx(5)
+        cx(5)
+        cast(1, 1)
+        qe(2, 0)
+        qe(2, 1)
+        qx(5)
+        m1(4, 0)
+        m1(4, 1)
+        sub(4, 0)
+        gmul(4, 0)
+        m2(2, 0)
+        sub(4, 1)
+        gmul(4, 1)
+        m1(4, 2)
+        gam(2, 0)
+        store_y(2, 0)
+        cast(2, 0)
+        m1(4, 3)
+        sub(4, 2)
+        m2(2, 1)
+        sub(4, 3)
+        gmul(4, 3)
+        vmulp(4, 2)
+        gam(2, 1)
+        store_y(2, 1)
+        te(3, 0)
+        ce(3, 0)
+        te(3, 1)
+        ce(3, 1)
+        ty(1, (0, 1))
+        cy(1, (0, 1))
+        cast(2, 1)
+        qy(0, 0)
+        qy(0, 1)
+        store_codes(0)
+        qe(3, 0)
+        qe(3, 1)
+        m1(5, 0)
+        m1(5, 1)
+        m1(5, 2)
+        m1(5, 3)
+        te(4, 0)
+        ce(4, 0)
+        te(4, 1)
+        ce(4, 1)
+        ty(2, (0, 1))
+        cy(2, (0, 1))
+        sub(5, 0)
+        gmul(5, 0)
+        m2(3, 0)
+        sub(5, 1)
+        gmul(5, 1)
+        m2(3, 1)
+        sub(5, 2)
+        sub(5, 3)
+        vmulp(5, 2)
+        vmulp(5, 3)
+        qe(4, 0)
+        qe(4, 1)
+        qy(1, 0)
+        qy(1, 1)
+        store_codes(1)
+        m2(4, 0)
+        gam(3, 0)
+        store_y(3, 0)
+        cast(3, 0)
+        gam(3, 1)
+        store_y(3, 1)
+        cast(3, 1)
+        qy(2, 0)
+        qy(2, 1)
+        store_codes(2)
+        te(5, 0)
+        ce(5, 0)
+        te(5, 1)
+        ce(5, 1)
+        ty(3, (0, 1))
+        cy(3, (0, 1))
+        m2(4, 1)
+        gam(4, 0)
+        store_y(4, 0)
+        qe(5, 0)
+        qe(5, 1)
+        cast(4, 0)
+        m2(5, 0)
+        gam(4, 1)
+        store_y(4, 1)
+        cast(4, 1)
+        qy(3, 0)
+        qy(3, 1)
+        store_codes(3)
+        ty(4, (0,))
+        cy(4, (0,))
+        m2(5, 1)
+        gam(5, 0)
+        store_y(5, 0)
+        qy(4, 0)
+        cast(5, 0)
+        ty(4, (1,))
+        cy(4, (1,))
+        gamb(5, 1)
+        gam(5, 1)
+        store_y(5, 1)
+        ty(5, (0,))
+        cy(5, (0,))
+        ty(5, (1,))
+        cy(5, (1,))
+        qy(4, 1)
+        store_codes(4)
+        qy(5, 0)
+        qy(5, 1)
+        store_codes(5)
+        store_plane(0, nc.sync)
+        store_plane(1, nc.scalar)
+        store_plane(2, nc.sync)
+        store_plane(3, nc.scalar)

@@ -95,9 +95,11 @@ def tile_feature_distillation_gradient_h1_kernel(
         def load_h(i, part=slice(0, F)):
             nc.sync.dma_start(out=h_sb[i][:, part], in_=h[rows(i), part])
 
-        def load_vectors():
-            nc.gpsimd.dma_start(out=lam_rows[:], in_=lam.rearrange("(c p t) -> p c t", p=P, t=4))
-            nc.gpsimd.dma_start(out=gamma_rows[:], in_=gamma.rearrange("(p t) -> p t", p=P))
+        def load_lam():
+            nc.scalar.dma_start(out=lam_rows[:], in_=lam.rearrange("(c p t) -> p c t", p=P, t=4))
+
+        def load_gamma():
+            nc.sync.dma_start(out=gamma_rows[:], in_=gamma.rearrange("(p t) -> p t", p=P))
 
         def turn(key, sources, bank=None):
             if bank is None:
@@ -108,7 +110,7 @@ def tile_feature_distillation_gradient_h1_kernel(
 
         def gather(key, groups):
             bank = held.pop(key)
-            grouped = work.tile([P, 2 * K], BF16, name="grouped", align_bytes=64, bufs=6)
+            grouped = work.tile([P, 2 * K], BF16, name="grouped", align_bytes=64, bufs=14)
             nc.scalar.copy(
                 out=grouped[:, : groups * K].bitcast(F32).rearrange("p (g m u) -> p g m u", g=groups, u=2),
                 in_=bank[:, : groups * 2 * P].rearrange("p (g u m) -> p g m u", g=groups, u=2),
@@ -173,7 +175,7 @@ def tile_feature_distillation_gradient_h1_kernel(
             held[("s1", i, c)] = bank
 
         def sub(i, c):
-            diff = work.tile([P, K], F32, name="diff", align_bytes=64, bufs=8)
+            diff = work.tile([P, K], F32, name="diff", align_bytes=64, bufs=10)
             nc.vector.tensor_tensor(
                 out=as_word_half(diff[:]),
                 in0=by_word_half(held.pop(("s1", i, c))[:]),
@@ -281,7 +283,7 @@ def tile_feature_distillation_gradient_h1_kernel(
         zero_plane(r_plane, cols(1))
         make_identity(nc, ident[:])
         load_x(0)
-        load_vectors()
+        load_lam()
         load_x(1)
         load_plane(p_plane, p_scales, cols(0, 2 * K), 0)
         load_plane(p_plane, p_scales, cols(0, 2 * K), 1)
@@ -300,6 +302,7 @@ def tile_feature_distillation_gradient_h1_kernel(
         load_x(2)
         load_codes(p_codes, p_words, cols(3, 2 * K))
         load_h(1, cols(1, 2 * K))
+        load_gamma()
         load_h(2, cols(0, 2 * K))
         load_x(3)
         load_h(2, cols(1, 2 * K))
@@ -319,221 +322,216 @@ def tile_feature_distillation_gradient_h1_kernel(
         load_h(4)
         load_h(5)
         txg(0, 0)
-        cxg(0, 0)
-        qxg(0, 0)
         txg(0, 1)
-        cxg(0, 1)
-        qxg(0, 1)
         tx(1)
-        cx(1)
+        cxg(0, 0)
         tc_lam(0)
-        cc_lam(0)
-        m1(0, 0)
+        cxg(0, 1)
+        qxg(0, 0)
+        cx(1)
+        qxg(0, 1)
         qx(1)
-        m1(1, 0)
-        tc_lam(1)
-        cc_lam(1)
+        m1(0, 0)
         m1(0, 1)
-        m1(1, 1)
+        m1(1, 0)
         sub(0, 0)
-        gmul(0, 0)
-        sub(1, 0)
-        gmul(1, 0)
-        m1(0, 2)
         sub(0, 1)
-        gmul(0, 1)
-        m1(1, 2)
-        sub(1, 1)
-        tx(2)
-        cx(2)
+        cc_lam(0)
+        sub(1, 0)
+        gmul(0, 0)
+        m1(1, 1)
+        m1(0, 2)
         m1(0, 3)
+        vmul(0, 1)
+        tc_lam(1)
         sub(0, 2)
-        m1(1, 3)
-        sub(1, 2)
-        vmulp(0, 2)
-        qx(2)
-        gmul(1, 1)
-        sub(0, 3)
-        vmulp(1, 2)
-        sub(1, 3)
-        gmul(1, 3)
-        vmulp(0, 3)
-        m1(2, 0)
-        m1(2, 1)
-        tx(3)
-        cx(3)
+        gmul(1, 0)
+        tx(2)
         te(0, 0)
+        sub(0, 3)
+        vmulp(0, 2)
+        tx(3)
+        vmulp(0, 3)
+        cx(2)
         ce(0, 0)
+        sub(1, 1)
+        cx(3)
+        m1(1, 2)
+        qx(2)
         te(0, 1)
-        ce(0, 1)
         tc_gamma()
-        cc_gamma()
-        sub(2, 0)
-        sub(2, 1)
-        m1(2, 2)
-        m1(2, 3)
-        qx(3)
+        m1(1, 3)
+        ce(0, 1)
+        m1(2, 0)
         qe(0, 0)
+        qx(3)
+        m1(2, 2)
+        sub(1, 2)
+        gmul(1, 1)
+        sub(1, 3)
+        sub(2, 0)
+        m1(2, 1)
         qe(0, 1)
-        gmul(2, 0)
-        gmul(2, 1)
-        sub(2, 2)
-        sub(2, 3)
-        gmul(2, 3)
-        vmulp(2, 2)
-        m2(0, 0)
+        m1(2, 3)
         m2(0, 1)
         te(1, 0)
-        ce(1, 0)
-        te(1, 1)
-        ce(1, 1)
+        vmulp(1, 3)
+        vmulp(1, 2)
         tx(4)
-        cx(4)
-        gam(0, 0)
-        store_y(0, 0)
-        cast(0, 0)
+        gmul(2, 0)
+        cc_gamma()
+        sub(2, 2)
+        sub(2, 3)
+        sub(2, 1)
+        vmulp(2, 2)
+        te(1, 1)
+        vmulp(2, 3)
         gam(0, 1)
         store_y(0, 1)
-        cast(0, 1)
-        qe(1, 0)
-        qe(1, 1)
-        qx(4)
-        m1(3, 0)
-        m1(3, 1)
-        sub(3, 0)
-        gmul(3, 0)
-        m2(1, 0)
-        sub(3, 1)
-        gmul(3, 1)
-        m1(3, 2)
-        gam(1, 0)
-        store_y(1, 0)
-        cast(1, 0)
+        cx(4)
         m1(3, 3)
-        sub(3, 2)
-        m2(1, 1)
+        m2(0, 0)
+        m1(3, 2)
+        ce(1, 1)
         sub(3, 3)
-        gmul(3, 3)
+        m1(3, 1)
+        ce(1, 0)
+        gam(0, 0)
+        store_y(0, 0)
+        m1(3, 0)
+        qe(1, 1)
+        qe(1, 0)
+        gmul(2, 1)
+        te(2, 1)
+        sub(3, 1)
+        qx(4)
+        te(2, 0)
+        gmul(3, 1)
+        sub(3, 2)
+        sub(3, 0)
         vmulp(3, 2)
+        tx(5)
+        ce(2, 0)
+        m2(1, 1)
         gam(1, 1)
         store_y(1, 1)
-        te(2, 0)
-        ce(2, 0)
-        te(2, 1)
-        ce(2, 1)
-        ty(0, (0, 1))
-        cy(0, (0, 1))
-        tx(5)
-        cx(5)
-        cast(1, 1)
-        qe(2, 0)
-        qe(2, 1)
-        qx(5)
-        m1(4, 0)
-        m1(4, 1)
-        sub(4, 0)
-        gmul(4, 0)
-        m2(2, 0)
-        sub(4, 1)
-        gmul(4, 1)
         m1(4, 2)
+        m2(1, 0)
+        cast(0, 1)
+        cx(5)
+        vmulp(3, 3)
+        sub(4, 2)
+        ce(2, 1)
+        m1(4, 3)
+        gam(1, 0)
+        store_y(1, 0)
+        qe(2, 0)
+        gmul(3, 0)
+        m1(4, 0)
+        te(3, 0)
+        cast(0, 0)
+        qe(2, 1)
+        cast(1, 0)
+        te(3, 1)
+        sub(4, 3)
+        ce(3, 1)
+        ty(0, (0, 1))
+        qx(5)
+        m2(2, 0)
+        sub(4, 0)
+        m1(4, 1)
+        m2(2, 1)
+        qe(3, 1)
+        m1(5, 0)
+        gmul(4, 0)
         gam(2, 0)
         store_y(2, 0)
-        cast(2, 0)
-        m1(4, 3)
-        sub(4, 2)
-        m2(2, 1)
-        sub(4, 3)
-        gmul(4, 3)
+        sub(4, 1)
+        m1(5, 2)
+        cy(0, (0, 1))
+        ce(3, 0)
         vmulp(4, 2)
         gam(2, 1)
         store_y(2, 1)
-        te(3, 0)
-        ce(3, 0)
-        te(3, 1)
-        ce(3, 1)
-        ty(1, (0, 1))
-        cy(1, (0, 1))
-        cast(2, 1)
-        qy(0, 0)
-        qy(0, 1)
-        store_codes(0)
-        qe(3, 0)
-        qe(3, 1)
-        m1(5, 0)
-        m1(5, 1)
-        m1(5, 2)
         m1(5, 3)
-        te(4, 0)
-        ce(4, 0)
-        te(4, 1)
-        ce(4, 1)
-        ty(2, (0, 1))
-        cy(2, (0, 1))
+        vmulp(4, 3)
+        m1(5, 1)
         sub(5, 0)
-        gmul(5, 0)
-        m2(3, 0)
-        sub(5, 1)
-        gmul(5, 1)
-        m2(3, 1)
+        cast(1, 1)
+        gmul(4, 1)
+        qe(3, 0)
         sub(5, 2)
+        cast(2, 0)
+        sub(5, 1)
+        te(4, 1)
+        te(4, 0)
+        gmul(5, 0)
         sub(5, 3)
+        gmul(5, 1)
+        ty(1, (0, 1))
+        m2(3, 0)
+        ce(4, 0)
+        ce(4, 1)
         vmulp(5, 2)
+        cast(2, 1)
         vmulp(5, 3)
         qe(4, 0)
+        m2(3, 1)
         qe(4, 1)
-        qy(1, 0)
-        qy(1, 1)
-        store_codes(1)
-        m2(4, 0)
-        gam(3, 0)
-        store_y(3, 0)
-        cast(3, 0)
+        ty(2, (0, 1))
         gam(3, 1)
         store_y(3, 1)
-        cast(3, 1)
+        cy(1, (0, 1))
+        cy(2, (0, 1))
+        te(5, 1)
+        gam(3, 0)
+        store_y(3, 0)
         qy(2, 0)
-        qy(2, 1)
-        store_codes(2)
         te(5, 0)
         ce(5, 0)
-        te(5, 1)
         ce(5, 1)
-        ty(3, (0, 1))
-        cy(3, (0, 1))
+        m2(4, 0)
+        qe(5, 0)
+        qy(1, 0)
+        qe(5, 1)
         m2(4, 1)
         gam(4, 0)
         store_y(4, 0)
-        qe(5, 0)
-        qe(5, 1)
-        cast(4, 0)
         m2(5, 0)
         gam(4, 1)
         store_y(4, 1)
-        cast(4, 1)
-        qy(3, 0)
-        qy(3, 1)
-        store_codes(3)
-        ty(4, (0,))
-        cy(4, (0,))
-        m2(5, 1)
+        qy(0, 1)
+        qy(2, 1)
+        store_codes(2)
         gam(5, 0)
         store_y(5, 0)
-        qy(4, 0)
-        cast(5, 0)
-        ty(4, (1,))
-        cy(4, (1,))
+        m2(5, 1)
+        cast(3, 0)
         gamb(5, 1)
+        cast(3, 1)
+        ty(3, (0, 1))
+        cast(4, 0)
+        qy(1, 1)
+        store_codes(1)
+        cast(4, 1)
+        qy(0, 0)
+        store_codes(0)
         gam(5, 1)
         store_y(5, 1)
-        ty(5, (0,))
-        cy(5, (0,))
-        ty(5, (1,))
-        cy(5, (1,))
+        cast(5, 0)
+        cy(3, (0, 1))
+        qy(3, 1)
+        ty(4, (0, 1))
+        qy(3, 0)
+        store_codes(3)
+        cy(4, (0, 1))
+        ty(5, (0, 1))
+        qy(4, 0)
         qy(4, 1)
         store_codes(4)
-        qy(5, 0)
+        cy(5, (0, 1))
         qy(5, 1)
+        qy(5, 0)
         store_codes(5)
         store_plane(0, nc.sync)
         store_plane(1, nc.scalar)

@@ -30,9 +30,7 @@ def tile_feature_distillation_gradient_h1_kernel(
     with ExitStack() as ctx:
         keep = ctx.enter_context(tc.tile_pool(name="keep", bufs=1))
         work = ctx.enter_context(tc.tile_pool(name="work", bufs=4))
-        sums = ctx.enter_context(tc.psum_pool(name="sums", bufs=4))
-        turns = ctx.enter_context(tc.psum_pool(name="turns", bufs=3))
-        fixed = ctx.enter_context(tc.psum_pool(name="fixed", bufs=1))
+        psum = ctx.enter_context(tc.psum_pool(name="psum", bufs=1))
         ctx.enter_context(tc.manual_schedule())
 
         def kept(name, shape, dtype):
@@ -49,8 +47,10 @@ def tile_feature_distillation_gradient_h1_kernel(
         gamma_rows = kept("gamma_rows", [P, 8], BF16)
         lam_all = kept("lam_all", [P, F], BF16)
         gamma_all = kept("gamma_all", [P, D], BF16)
-        x_codes = [kept("x_codes%d" % i, [P, GD * P], U32) for i in range(TILES)]
-        x_plane = [kept("x_plane%d" % i, [P, GD * P], U8) for i in range(TILES)]
+        x_grouped = kept("x_grouped", [P, TILES * D], BF16)
+        x_codes = kept("x_codes", [P, TILES * GD * P], U32)
+        x_plane = kept("x_plane", [P, TILES * GD * P], U8)
+        y_grouped = kept("y_grouped", [P, GD, 4 * M], BF16)
         e_codes = [kept("e_codes%d" % i, [P, GF * P], U32) for i in range(TILES)]
         e_plane = [kept("e_plane%d" % i, [P, GF * P], U8) for i in range(TILES)]
         e_bf = [kept("e_bf%d" % i, [P, F], BF16) for i in range(TILES)]
@@ -59,8 +59,24 @@ def tile_feature_distillation_gradient_h1_kernel(
         y_codes = kept("y_codes", [P, GD, M], U32)
         y_plane = kept("y_plane", [P, GD, M], U8)
 
-        lam_bank = fixed.tile([P, 4 * P], F32, name="lam_bank")
+        lam_bank = psum.tile([P, K], F32, name="lam_bank")
+        e_grouped = [kept("e_grouped%d" % i, [P, F], BF16) for i in range(TILES)]
+        free_banks = list(range(7))
+        bank_of = {}
+
+        def take_bank(key):
+            k = free_banks[0]
+            free_banks.remove(k)
+            bank_of[key] = k
+            held[key] = psum.tile([P, K], F32, name="bank%d" % k)
+            return held[key]
+
+        def give_bank(key):
+            free_banks.append(bank_of[key])
+            return held[key]
+
         held = {}
+        diffs = {}
 
         def rows(i):
             return slice(i * P, (i + 1) * P)
@@ -89,8 +105,8 @@ def tile_feature_distillation_gradient_h1_kernel(
                 in_=words[:, :, part].rearrange("g p n -> p g n").bitcast(I32),
             )
 
-        def load_x(i):
-            nc.sync.dma_start(out=x_sb[i][:], in_=x[rows(i), :])
+        def load_x(i, part=slice(0, D)):
+            nc.sync.dma_start(out=x_sb[i][:, part], in_=x[rows(i), part])
 
         def load_h(i, part=slice(0, F)):
             nc.sync.dma_start(out=h_sb[i][:, part], in_=h[rows(i), part])
@@ -103,26 +119,24 @@ def tile_feature_distillation_gradient_h1_kernel(
 
         def turn(key, sources, bank=None):
             if bank is None:
-                bank = turns.tile([P, 4 * P], F32, name="turn_bank")
+                bank = take_bank(key)
             for j, source in enumerate(sources):
                 nc.tensor.transpose(bank[:, cols(j, P)], source, ident[:])
             held[key] = bank
 
-        def gather(key, groups):
-            bank = held.pop(key)
-            grouped = work.tile([P, 2 * K], BF16, name="grouped", align_bytes=64, bufs=14)
-            nc.scalar.copy(
-                out=grouped[:, : groups * K].bitcast(F32).rearrange("p (g m u) -> p g m u", g=groups, u=2),
+        def gather(key, groups, target, copy):
+            bank = give_bank(key)
+            copy(
+                out=target.bitcast(F32).rearrange("p g (m u) -> p g m u", u=2),
                 in_=bank[:, : groups * 2 * P].rearrange("p (g u m) -> p g m u", g=groups, u=2),
             )
-            held[key + ("grouped",)] = grouped
 
         def tc_lam(half):
             words = lam_rows[:].rearrange("p c t -> p (c t)").bitcast(F32)
             turn(("lam", half), [words[:, j : j + 1].to_broadcast([P, P]) for j in range(4 * half, 4 * half + 4)], lam_bank if half == 1 else None)
 
         def cc_lam(half):
-            nc.scalar.copy(out=lam_all[:, cols(half, 2 * K)].bitcast(F32), in_=held.pop(("lam", half))[:])
+            nc.scalar.copy(out=lam_all[:, cols(half, 2 * K)].bitcast(F32), in_=(lam_bank if half == 1 else give_bank(("lam", half)))[:])
 
         def tc_gamma():
             words = gamma_rows[:].bitcast(F32)
@@ -131,7 +145,7 @@ def tile_feature_distillation_gradient_h1_kernel(
         def cc_gamma():
             nc.scalar.copy(
                 out=gamma_all[:].bitcast(F32).rearrange("q (p j) -> q p j", j=4),
-                in_=held.pop(("gamma",))[:].rearrange("q (j p) -> q p j", j=4),
+                in_=give_bank(("gamma",))[:].rearrange("q (j p) -> q p j", j=4),
             )
 
         def tx(i):
@@ -142,51 +156,60 @@ def tile_feature_distillation_gradient_h1_kernel(
             words = x_sb[i][:].bitcast(F32)
             turn(("x", i, g), [words[:, 256 * g + u : 256 * (g + 1) : 2] for u in range(2)])
 
+        def x_target(first, count):
+            return x_grouped[:, first * K : (first + count) * K].rearrange("p (g n) -> p g n", g=count)
+
         def cxg(i, g):
-            gather(("x", i, g), 1)
+            gather(("x", i, g), 1, x_target(GD * i + g, 1), nc.scalar.copy)
+
+        def cxv(i, g):
+            gather(("x", i, g), 1, x_target(GD * i + g, 1), nc.vector.tensor_copy)
+
+        def quantize_x(first, count):
+            nc.vector.quantize_mx(
+                out=x_codes[:, first * P : (first + count) * P].bitcast(FP8X4),
+                scales=x_plane[:, first * P : (first + count) * P],
+                in_=x_grouped[:, first * K : (first + count) * K],
+            )
 
         def qxg(i, g):
-            nc.vector.quantize_mx(
-                out=x_codes[i][:, cols(g, P)].bitcast(FP8X4),
-                scales=x_plane[i][:, cols(g, P)],
-                in_=held.pop(("x", i, g, "grouped"))[:, :K],
-            )
+            quantize_x(GD * i + g, 1)
 
         def cx(i):
-            gather(("x", i), 2)
+            gather(("x", i), GD, x_target(GD * i, GD), nc.scalar.copy)
 
         def qx(i):
-            nc.vector.quantize_mx(
-                out=x_codes[i][:].bitcast(FP8X4), scales=x_plane[i][:], in_=held.pop(("x", i, "grouped"))[:]
-            )
+            quantize_x(GD * i, GD)
+
+        def qxr(i, n):
+            quantize_x(GD * i, GD * n)
 
         def m1(i, c):
-            bank = sums.tile([P, K], F32, name="sum_bank")
+            bank = take_bank(("s1", i, c))
             for g in range(GD):
                 nc.tensor.matmul_mx(
                     out=bank[:],
-                    lhsT=x_codes[i][:, cols(g, P)].bitcast(FP8X4),
-                    lhsT_scale=x_plane[i][:, cols(g, P)],
+                    lhsT=x_codes[:, cols(GD * i + g, P)].bitcast(FP8X4),
+                    lhsT_scale=x_plane[:, cols(GD * i + g, P)],
                     rhs=p_codes[:, g, cols(c, 2 * K)].bitcast(FP4X4),
                     rhs_scale=p_plane[:, g, cols(c)],
                     start=(g == 0),
                     stop=(g == GD - 1),
                 )
-            held[("s1", i, c)] = bank
 
         def sub(i, c):
-            diff = work.tile([P, K], F32, name="diff", align_bytes=64, bufs=10)
+            if (i, c // 2) not in diffs:
+                diffs[(i, c // 2)] = work.tile([P, 2 * K], F32, name="diff", align_bytes=64, bufs=7)
+            diff = diffs[(i, c // 2)][:, cols(c % 2)]
+            bank = give_bank(("s1", i, c))
             nc.vector.tensor_tensor(
-                out=as_word_half(diff[:]),
-                in0=by_word_half(held.pop(("s1", i, c))[:]),
-                in1=by_word_half(h_sb[i][:, cols(c)]),
-                op=SUB,
+                out=as_word_half(diff), in0=by_word_half(bank[:]), in1=by_word_half(h_sb[i][:, cols(c)]), op=SUB
             )
             held[("diff", i, c)] = diff
 
         def mul(engine, i, c):
             engine.tensor_tensor(
-                out=e_bf[i][:, cols(c)], in0=held.pop(("diff", i, c))[:], in1=lam_all[:, cols(c)], op=MULT
+                out=e_bf[i][:, cols(c)], in0=held.pop(("diff", i, c)), in1=lam_all[:, cols(c)], op=MULT
             )
 
         def gmul(i, c):
@@ -198,9 +221,14 @@ def tile_feature_distillation_gradient_h1_kernel(
         def vmulp(i, c):
             nc.vector.tensor_tensor(
                 out=e_bf[i][:, cols(c)],
-                in0=held.pop(("diff", i, c))[:],
+                in0=held.pop(("diff", i, c)),
                 in1=lam_bank[:].bitcast(BF16)[:, cols(c - 2)],
                 op=MULT,
+            )
+
+        def vm2(i):
+            nc.vector.tensor_tensor(
+                out=e_bf[i][:, cols(1, 2 * K)], in0=diffs[(i, 1)][:], in1=lam_bank[:].bitcast(BF16), op=MULT
             )
 
         def te(i, half):
@@ -208,17 +236,33 @@ def tile_feature_distillation_gradient_h1_kernel(
             turn(("e", i, half), [words[:, cols(j, P)] for j in range(4 * half, 4 * half + 4)])
 
         def ce(i, half):
-            gather(("e", i, half), 2)
+            target = e_grouped[i][:, cols(half, 2 * K)].rearrange("p (g n) -> p g n", g=2)
+            gather(("e", i, half), 2, target, nc.scalar.copy)
 
         def qe(i, half):
             nc.vector.quantize_mx(
                 out=e_codes[i][:, cols(half, 2 * P)].bitcast(FP8X4),
                 scales=e_plane[i][:, cols(half, 2 * P)],
-                in_=held.pop(("e", i, half, "grouped"))[:],
+                in_=e_grouped[i][:, cols(half, 2 * K)],
             )
 
+        def qe2(i):
+            nc.vector.quantize_mx(out=e_codes[i][:].bitcast(FP8X4), scales=e_plane[i][:], in_=e_grouped[i][:])
+
+        def px(i):
+            words = work.tile([P, K], F32, name="x_words", bufs=2)
+            nc.scalar.copy(
+                out=words[:].rearrange("m (g u p) -> m g u p", g=GD, u=2),
+                in_=x_sb[i][:].bitcast(F32).rearrange("m (g p u) -> m g u p", g=GD, u=2),
+            )
+            held[("x_words", i)] = words
+
+        def tp(i):
+            words = held.pop(("x_words", i))
+            turn(("x", i), [words[:, cols(j, P)] for j in range(4)])
+
         def m2(i, d):
-            bank = sums.tile([P, K], F32, name="sum_bank")
+            bank = take_bank(("s2", i, d))
             for g in range(GF):
                 nc.tensor.matmul_mx(
                     out=bank[:],
@@ -229,11 +273,10 @@ def tile_feature_distillation_gradient_h1_kernel(
                     start=(g == 0),
                     stop=(g == GF - 1),
                 )
-            held[("s2", i, d)] = bank
 
         def gam(i, d):
             nc.vector.tensor_tensor(
-                out=y_f32[i][:, cols(d)], in0=held.pop(("s2", i, d))[:], in1=gamma_all[:, cols(d)], op=MULT
+                out=y_f32[i][:, cols(d)], in0=give_bank(("s2", i, d))[:], in1=gamma_all[:, cols(d)], op=MULT
             )
 
         def gamb(i, d):
@@ -254,21 +297,26 @@ def tile_feature_distillation_gradient_h1_kernel(
             words = y_bf[i][:].bitcast(F32)
             turn(("y", i, ds), [words[:, cols(2 * d + u, P)] for d in ds for u in range(2)])
 
-        def cy(i, ds):
-            gather(("y", i, ds), len(ds))
-            grouped = held.pop(("y", i, ds, "grouped"))
-            for j, d in enumerate(ds):
-                held[("yg", i, d)] = grouped[:, cols(j)]
+        def cyv(i, ds):
+            cy(i, ds, nc.vector.tensor_copy)
 
-        def qy(i, d):
+        def cy(i, ds, copy=nc.scalar.copy):
+            gather(("y", i, ds), len(ds), y_grouped[:, ds[0] : ds[-1] + 1, cols(i, 4 * P)], copy)
+
+        def qyr(d, i, n):
             nc.vector.quantize_mx(
-                out=y_codes[:, d, rows(i)].bitcast(FP8X4), scales=y_plane[:, d, rows(i)], in_=held.pop(("yg", i, d))
+                out=y_codes[:, d, i * P : (i + n) * P].bitcast(FP8X4),
+                scales=y_plane[:, d, i * P : (i + n) * P],
+                in_=y_grouped[:, d, 4 * i * P : 4 * (i + n) * P],
             )
 
-        def store_codes(i, part=slice(0, GD)):
+        def qy(i, d):
+            qyr(d, i, 1)
+
+        def store_codes(i, n, part=slice(0, GD)):
             nc.sync.dma_start(
-                out=out_1.rearrange("g p m t -> p g (m t)")[:, part, cols(i, 4 * P)].bitcast(I32),
-                in_=y_codes[:, part, rows(i)].bitcast(I32),
+                out=out_1.rearrange("g p m t -> p g (m t)")[:, part, 4 * i * P : 4 * (i + n) * P].bitcast(I32),
+                in_=y_codes[:, part, i * P : (i + n) * P].bitcast(I32),
             )
 
         def store_plane(r, engine):
@@ -277,262 +325,259 @@ def tile_feature_distillation_gradient_h1_kernel(
                 in_=y_plane[r:P:32, :, :].bitcast(I32),
             )
 
-        zero_plane(p_plane, cols(0, 2 * K))
-        zero_plane(p_plane, cols(1, 2 * K))
-        zero_plane(r_plane, cols(0))
-        zero_plane(r_plane, cols(1))
         make_identity(nc, ident[:])
-        load_x(0)
-        load_lam()
+        load_x(0, cols(0))
+        txg(0, 0)
+        load_x(0, cols(1))
+        txg(0, 1)
         load_x(1)
+        load_lam()
+        tx(1)
+        zero_plane(p_plane, cols(0, 2 * K))
+        load_codes(p_codes, p_words, cols(0, 2 * K))
+        cxv(0, 0)
         load_plane(p_plane, p_scales, cols(0, 2 * K), 0)
         load_plane(p_plane, p_scales, cols(0, 2 * K), 1)
         load_plane(p_plane, p_scales, cols(0, 2 * K), 2)
         load_plane(p_plane, p_scales, cols(0, 2 * K), 3)
-        load_codes(p_codes, p_words, cols(0, 2 * K))
-        load_h(0, cols(0, 2 * K))
+        load_x(2)
         load_codes(p_codes, p_words, cols(1, 2 * K))
+        zero_plane(p_plane, cols(1, 2 * K))
+        cxg(0, 1)
+        cx(1)
+        load_gamma()
+        tc_lam(0)
+        px(2)
+        qxg(0, 0)
+        qxg(0, 1)
+        load_h(0, cols(0, 2 * K))
+        m1(0, 0)
         load_h(1, cols(0, 2 * K))
         load_plane(p_plane, p_scales, cols(1, 2 * K), 0)
         load_plane(p_plane, p_scales, cols(1, 2 * K), 1)
         load_plane(p_plane, p_scales, cols(1, 2 * K), 2)
         load_plane(p_plane, p_scales, cols(1, 2 * K), 3)
+        zero_plane(r_plane, cols(0))
+        cc_lam(0)
+        tp(2)
         load_codes(p_codes, p_words, cols(2, 2 * K))
-        load_h(0, cols(1, 2 * K))
-        load_x(2)
+        qx(1)
         load_codes(p_codes, p_words, cols(3, 2 * K))
-        load_h(1, cols(1, 2 * K))
-        load_gamma()
-        load_h(2, cols(0, 2 * K))
+        cx(2)
+        sub(0, 0)
+        m1(1, 0)
+        m1(0, 1)
+        zero_plane(r_plane, cols(1))
+        m1(1, 1)
+        m1(0, 2)
+        m1(0, 3)
+        m1(1, 2)
+        sub(1, 0)
+        sub(0, 1)
+        qx(2)
+        load_h(0, cols(1, 2 * K))
+        gmul(0, 0)
         load_x(3)
+        load_h(1, cols(1, 2 * K))
+        load_x(4)
+        sub(1, 1)
+        sub(0, 2)
+        load_h(2, cols(0, 2 * K))
+        gmul(0, 1)
+        m1(1, 3)
+        load_x(5)
+        tc_lam(1)
+        gmul(1, 0)
+        sub(0, 3)
+        tc_gamma()
+        px(3)
+        gmul(1, 1)
+        tp(3)
+        te(0, 0)
+        px(4)
+        cx(3)
+        sub(1, 2)
+        load_codes(r_codes, r_words, cols(0, 2 * K))
+        cc_lam(1)
+        m1(2, 0)
         load_h(2, cols(1, 2 * K))
-        load_plane(r_plane, r_scales, cols(0), 0)
-        load_plane(r_plane, r_scales, cols(0), 1)
-        load_plane(r_plane, r_scales, cols(0), 2)
-        load_plane(r_plane, r_scales, cols(0), 3)
+        m1(2, 1)
+        vmulp(0, 2)
+        vmulp(0, 3)
+        sub(1, 3)
+        ce(0, 0)
+        m1(2, 2)
         load_plane(r_plane, r_scales, cols(1), 0)
         load_plane(r_plane, r_scales, cols(1), 1)
         load_plane(r_plane, r_scales, cols(1), 2)
         load_plane(r_plane, r_scales, cols(1), 3)
-        load_codes(r_codes, r_words, cols(0, 2 * K))
-        load_codes(r_codes, r_words, cols(1, 2 * K))
-        load_x(4)
-        load_h(3)
-        load_x(5)
-        load_h(4)
-        load_h(5)
-        txg(0, 0)
-        txg(0, 1)
-        tx(1)
-        cxg(0, 0)
-        tc_lam(0)
-        cxg(0, 1)
-        qxg(0, 0)
-        cx(1)
-        qxg(0, 1)
-        qx(1)
-        m1(0, 0)
-        m1(0, 1)
-        m1(1, 0)
-        sub(0, 0)
-        sub(0, 1)
-        cc_lam(0)
-        sub(1, 0)
-        gmul(0, 0)
-        m1(1, 1)
-        m1(0, 2)
-        m1(0, 3)
-        vmul(0, 1)
-        tc_lam(1)
-        sub(0, 2)
-        gmul(1, 0)
-        tx(2)
-        te(0, 0)
-        sub(0, 3)
-        vmulp(0, 2)
-        tx(3)
-        vmulp(0, 3)
-        cx(2)
-        ce(0, 0)
-        sub(1, 1)
-        cx(3)
-        m1(1, 2)
-        qx(2)
-        te(0, 1)
-        tc_gamma()
-        m1(1, 3)
-        ce(0, 1)
-        m1(2, 0)
-        qe(0, 0)
-        qx(3)
-        m1(2, 2)
-        sub(1, 2)
-        gmul(1, 1)
-        sub(1, 3)
         sub(2, 0)
-        m1(2, 1)
-        qe(0, 1)
         m1(2, 3)
-        m2(0, 1)
-        te(1, 0)
-        vmulp(1, 3)
-        vmulp(1, 2)
-        tx(4)
-        gmul(2, 0)
-        cc_gamma()
-        sub(2, 2)
-        sub(2, 3)
+        qx(3)
+        px(5)
+        te(0, 1)
         sub(2, 1)
-        vmulp(2, 2)
-        te(1, 1)
-        vmulp(2, 3)
-        gam(0, 1)
-        store_y(0, 1)
+        cc_gamma()
+        tp(4)
+        sub(2, 2)
+        tp(5)
+        vmulp(1, 2)
+        vmulp(1, 3)
+        te(1, 0)
+        gmul(2, 0)
         cx(4)
-        m1(3, 3)
-        m2(0, 0)
-        m1(3, 2)
-        ce(1, 1)
-        sub(3, 3)
-        m1(3, 1)
-        ce(1, 0)
-        gam(0, 0)
-        store_y(0, 0)
         m1(3, 0)
-        qe(1, 1)
-        qe(1, 0)
-        gmul(2, 1)
-        te(2, 1)
-        sub(3, 1)
-        qx(4)
-        te(2, 0)
-        gmul(3, 1)
-        sub(3, 2)
-        sub(3, 0)
-        vmulp(3, 2)
-        tx(5)
-        ce(2, 0)
-        m2(1, 1)
-        gam(1, 1)
-        store_y(1, 1)
-        m1(4, 2)
-        m2(1, 0)
-        cast(0, 1)
+        ce(0, 1)
         cx(5)
-        vmulp(3, 3)
-        sub(4, 2)
-        ce(2, 1)
-        m1(4, 3)
-        gam(1, 0)
-        store_y(1, 0)
-        qe(2, 0)
+        sub(2, 3)
+        ce(1, 0)
+        m1(3, 1)
+        m1(3, 2)
+        qe2(0)
+        m1(3, 3)
+        gmul(2, 1)
+        te(1, 1)
+        ce(1, 1)
+        load_h(3)
+        te(2, 0)
+        sub(3, 0)
+        ce(2, 0)
+        qxr(4, 2)
+        vmulp(2, 2)
+        load_plane(r_plane, r_scales, cols(0), 0)
+        load_plane(r_plane, r_scales, cols(0), 1)
+        load_plane(r_plane, r_scales, cols(0), 2)
+        load_plane(r_plane, r_scales, cols(0), 3)
+        vmulp(2, 3)
+        m2(0, 0)
+        load_h(5)
         gmul(3, 0)
         m1(4, 0)
-        te(3, 0)
-        cast(0, 0)
-        qe(2, 1)
-        cast(1, 0)
-        te(3, 1)
-        sub(4, 3)
-        ce(3, 1)
-        ty(0, (0, 1))
-        qx(5)
-        m2(2, 0)
-        sub(4, 0)
+        sub(3, 1)
+        qe2(1)
         m1(4, 1)
-        m2(2, 1)
-        qe(3, 1)
+        m1(4, 2)
+        load_codes(r_codes, r_words, cols(1, 2 * K))
+        sub(3, 2)
+        load_h(4)
+        sub(3, 3)
+        sub(4, 0)
+        gam(0, 0)
+        store_y(0, 0)
+        sub(4, 1)
+        m2(0, 1)
+        m1(4, 3)
+        m2(1, 0)
+        gam(0, 1)
+        store_y(0, 1)
+        te(2, 1)
+        sub(4, 2)
+        gam(1, 0)
+        store_y(1, 0)
+        gmul(3, 1)
+        vmulp(3, 2)
+        cast(0, 0)
+        gmul(3, 3)
+        ce(2, 1)
+        te(3, 0)
+        m2(1, 1)
         m1(5, 0)
+        cast(0, 1)
+        m1(5, 1)
+        sub(4, 3)
         gmul(4, 0)
+        ce(3, 0)
+        te(3, 1)
+        gmul(4, 1)
+        sub(5, 0)
+        qe2(2)
+        ty(0, (0, 1))
+        cast(1, 0)
+        cy(0, (0, 1))
+        gam(1, 1)
+        store_y(1, 1)
+        te(4, 0)
+        ce(3, 1)
+        sub(5, 1)
+        m1(5, 2)
+        vmulp(4, 2)
+        vmulp(4, 3)
+        gmul(5, 0)
+        sub(5, 2)
+        cast(1, 1)
+        m1(5, 3)
+        qe2(3)
+        m2(2, 0)
+        m2(2, 1)
+        ce(4, 0)
+        gmul(5, 1)
+        te(4, 1)
         gam(2, 0)
         store_y(2, 0)
-        sub(4, 1)
-        m1(5, 2)
-        cy(0, (0, 1))
-        ce(3, 0)
-        vmulp(4, 2)
+        ty(1, (0, 1))
+        sub(5, 3)
         gam(2, 1)
         store_y(2, 1)
-        m1(5, 3)
-        vmulp(4, 3)
-        m1(5, 1)
-        sub(5, 0)
-        cast(1, 1)
-        gmul(4, 1)
-        qe(3, 0)
-        sub(5, 2)
-        cast(2, 0)
-        sub(5, 1)
-        te(4, 1)
-        te(4, 0)
-        gmul(5, 0)
-        sub(5, 3)
-        gmul(5, 1)
-        ty(1, (0, 1))
-        m2(3, 0)
-        ce(4, 0)
         ce(4, 1)
-        vmulp(5, 2)
-        cast(2, 1)
-        vmulp(5, 3)
-        qe(4, 0)
-        m2(3, 1)
-        qe(4, 1)
-        ty(2, (0, 1))
-        gam(3, 1)
-        store_y(3, 1)
-        cy(1, (0, 1))
-        cy(2, (0, 1))
-        te(5, 1)
-        gam(3, 0)
-        store_y(3, 0)
-        qy(2, 0)
+        cast(2, 0)
         te(5, 0)
         ce(5, 0)
-        ce(5, 1)
-        m2(4, 0)
+        m2(3, 0)
+        m2(3, 1)
+        gmul(5, 2)
+        cast(2, 1)
+        vmulp(5, 3)
+        qe2(4)
+        gam(3, 0)
+        store_y(3, 0)
+        cy(1, (0, 1))
+        gam(3, 1)
+        store_y(3, 1)
+        te(5, 1)
+        ty(2, (0, 1))
         qe(5, 0)
-        qy(1, 0)
-        qe(5, 1)
-        m2(4, 1)
+        ce(5, 1)
+        cast(3, 0)
+        m2(4, 0)
+        cast(3, 1)
         gam(4, 0)
         store_y(4, 0)
-        m2(5, 0)
+        cy(2, (0, 1))
+        qe(5, 1)
+        m2(4, 1)
+        ty(3, (0, 1))
         gam(4, 1)
         store_y(4, 1)
-        qy(0, 1)
-        qy(2, 1)
-        store_codes(2)
+        cast(4, 0)
+        m2(5, 0)
+        qyr(0, 0, 2)
+        qyr(1, 0, 2)
+        store_codes(0, 2)
+        cy(3, (0, 1))
         gam(5, 0)
         store_y(5, 0)
         m2(5, 1)
-        cast(3, 0)
-        gamb(5, 1)
-        cast(3, 1)
-        ty(3, (0, 1))
-        cast(4, 0)
-        qy(1, 1)
-        store_codes(1)
+        qyr(0, 2, 2)
+        qyr(1, 2, 2)
+        store_codes(2, 2)
         cast(4, 1)
-        qy(0, 0)
-        store_codes(0)
+        cast(5, 0)
+        ty(4, (0, 1))
+        ty(5, (0,))
+        cy(4, (0, 1))
+        gamb(5, 1)
         gam(5, 1)
         store_y(5, 1)
-        cast(5, 0)
-        cy(3, (0, 1))
-        qy(3, 1)
-        ty(4, (0, 1))
-        qy(3, 0)
-        store_codes(3)
-        cy(4, (0, 1))
-        ty(5, (0, 1))
-        qy(4, 0)
-        qy(4, 1)
-        store_codes(4)
-        cy(5, (0, 1))
-        qy(5, 1)
+        cy(5, (0,))
+        qyr(0, 4, 1)
+        qyr(1, 4, 1)
+        store_codes(4, 1)
+        ty(5, (1,))
+        cyv(5, (1,))
         qy(5, 0)
-        store_codes(5)
+        qy(5, 1)
+        store_codes(5, 1, slice(0, 1))
+        store_codes(5, 1, slice(1, 2))
         store_plane(0, nc.sync)
         store_plane(1, nc.scalar)
         store_plane(2, nc.sync)

@@ -21,6 +21,7 @@ K = 512
 TILES = M // P
 GD = D // K
 GF = F // K
+Y_GROUPS = ((0, 2), (2, 2), (4, 1), (5, 1))
 
 
 def tile_feature_distillation_gradient_h1_kernel(
@@ -39,10 +40,10 @@ def tile_feature_distillation_gradient_h1_kernel(
         ident = kept("ident", [P, P], F32)
         x_sb = [kept("x%d" % i, [P, D], BF16) for i in range(TILES)]
         h_sb = [kept("h%d" % i, [P, F], BF16) for i in range(TILES)]
-        p_codes = kept("p_codes", [P, GD, 2 * F], U8)
-        p_plane = kept("p_plane", [P, GD, F], U8)
-        r_codes = kept("r_codes", [P, GF, 2 * D], U8)
-        r_plane = kept("r_plane", [P, GF, D], U8)
+        p_codes = [kept("p_codes%d" % c, [P, GD, 2 * K], U8) for c in range(GF)]
+        p_plane = [kept("p_plane%d" % a, [P, GD, 2 * K], U8) for a in range(2)]
+        r_codes = [kept("r_codes%d" % d, [P, GF, 2 * K], U8) for d in range(GD)]
+        r_plane = [kept("r_plane%d" % d, [P, GF, K], U8) for d in range(GD)]
         lam_rows = kept("lam_rows", [P, GF, 4], BF16)
         gamma_rows = kept("gamma_rows", [P, 8], BF16)
         lam_all = kept("lam_all", [P, F], BF16)
@@ -50,13 +51,19 @@ def tile_feature_distillation_gradient_h1_kernel(
         x_grouped = kept("x_grouped", [P, TILES * D], BF16)
         x_codes = kept("x_codes", [P, TILES * GD * P], U32)
         x_plane = kept("x_plane", [P, TILES * GD * P], U8)
-        y_grouped = kept("y_grouped", [P, GD, 4 * M], BF16)
         e_codes = [kept("e_codes%d" % i, [P, GF * P], U32) for i in range(TILES)]
         e_plane = [kept("e_plane%d" % i, [P, GF * P], U8) for i in range(TILES)]
         e_bf = [kept("e_bf%d" % i, [P, F], BF16) for i in range(TILES)]
         y_f32 = [kept("y_f32_%d" % i, [P, D], F32) for i in range(TILES)]
         y_bf = [kept("y_bf%d" % i, [P, D], BF16) for i in range(TILES)]
-        y_codes = kept("y_codes", [P, GD, M], U32)
+        y_grouped = {}
+        y_codes = {}
+        for first, count in Y_GROUPS:
+            grouped = kept("y_grouped%d" % first, [P, GD, 4 * P * count], BF16)
+            codes = kept("y_codes%d" % first, [P, GD, P * count], U32)
+            for j in range(count):
+                y_grouped[first + j] = (grouped, j)
+            y_codes[first] = codes
         y_plane = kept("y_plane", [P, GD, M], U8)
 
         lam_bank = psum.tile([P, K], F32, name="lam_bank")
@@ -90,19 +97,20 @@ def tile_feature_distillation_gradient_h1_kernel(
         def as_word_half(ap):
             return ap.rearrange("m (u p e) -> m u p e", u=2, e=2)
 
-        def zero_plane(plane, part):
-            nc.vector.memset(plane[:, :, part].bitcast(I32), 0)
+        def zero_plane(planes, a):
+            nc.vector.memset(planes[a][:].rearrange("p g n -> p (g n)").bitcast(I32), 0)
 
-        def load_plane(plane, scales, part, r):
+        def load_plane(planes, scales, a, r):
+            width = planes[a].shape[2]
             nc.sync.dma_start(
-                out=plane[r:P:32, :, part].bitcast(I32),
-                in_=scales[:, r:16:4, part].rearrange("g q n -> q g n").bitcast(I32),
+                out=planes[a][r:P:32, :, :].bitcast(I32),
+                in_=scales[:, r:16:4, cols(a, width)].rearrange("g q n -> q g n").bitcast(I32),
             )
 
-        def load_codes(codes, words, part):
+        def load_codes(codes, words, c):
             nc.sync.dma_start(
-                out=codes[:, :, part].bitcast(I32),
-                in_=words[:, :, part].rearrange("g p n -> p g n").bitcast(I32),
+                out=codes[c][:].bitcast(I32),
+                in_=words[:, :, cols(c, 2 * K)].rearrange("g p n -> p g n").bitcast(I32),
             )
 
         def load_x(i, part=slice(0, D)):
@@ -191,15 +199,15 @@ def tile_feature_distillation_gradient_h1_kernel(
                     out=bank[:],
                     lhsT=x_codes[:, cols(GD * i + g, P)].bitcast(FP8X4),
                     lhsT_scale=x_plane[:, cols(GD * i + g, P)],
-                    rhs=p_codes[:, g, cols(c, 2 * K)].bitcast(FP4X4),
-                    rhs_scale=p_plane[:, g, cols(c)],
+                    rhs=p_codes[c][:, g, :].bitcast(FP4X4),
+                    rhs_scale=p_plane[c // 2][:, g, cols(c % 2)],
                     start=(g == 0),
                     stop=(g == GD - 1),
                 )
 
         def sub(i, c):
             if (i, c // 2) not in diffs:
-                diffs[(i, c // 2)] = work.tile([P, 2 * K], F32, name="diff", align_bytes=64, bufs=7)
+                diffs[(i, c // 2)] = work.tile([P, 2 * K], F32, name="diff", align_bytes=64, bufs=5)
             diff = diffs[(i, c // 2)][:, cols(c % 2)]
             bank = give_bank(("s1", i, c))
             nc.vector.tensor_tensor(
@@ -250,7 +258,7 @@ def tile_feature_distillation_gradient_h1_kernel(
             nc.vector.quantize_mx(out=e_codes[i][:].bitcast(FP8X4), scales=e_plane[i][:], in_=e_grouped[i][:])
 
         def px(i):
-            words = work.tile([P, K], F32, name="x_words", bufs=2)
+            words = work.tile([P, K], F32, name="x_words", bufs=4)
             nc.scalar.copy(
                 out=words[:].rearrange("m (g u p) -> m g u p", g=GD, u=2),
                 in_=x_sb[i][:].bitcast(F32).rearrange("m (g p u) -> m g u p", g=GD, u=2),
@@ -268,8 +276,8 @@ def tile_feature_distillation_gradient_h1_kernel(
                     out=bank[:],
                     lhsT=e_codes[i][:, cols(g, P)].bitcast(FP8X4),
                     lhsT_scale=e_plane[i][:, cols(g, P)],
-                    rhs=r_codes[:, g, cols(d, 2 * K)].bitcast(FP4X4),
-                    rhs_scale=r_plane[:, g, cols(d)],
+                    rhs=r_codes[d][:, g, :].bitcast(FP4X4),
+                    rhs_scale=r_plane[d][:, g, :],
                     start=(g == 0),
                     stop=(g == GF - 1),
                 )
@@ -301,13 +309,14 @@ def tile_feature_distillation_gradient_h1_kernel(
             cy(i, ds, nc.vector.tensor_copy)
 
         def cy(i, ds, copy=nc.scalar.copy):
-            gather(("y", i, ds), len(ds), y_grouped[:, ds[0] : ds[-1] + 1, cols(i, 4 * P)], copy)
+            grouped, j = y_grouped[i]
+            gather(("y", i, ds), len(ds), grouped[:, ds[0] : ds[-1] + 1, cols(j, 4 * P)], copy)
 
         def qyr(d, i, n):
             nc.vector.quantize_mx(
-                out=y_codes[:, d, i * P : (i + n) * P].bitcast(FP8X4),
+                out=y_codes[i][:, d, :].bitcast(FP8X4),
                 scales=y_plane[:, d, i * P : (i + n) * P],
-                in_=y_grouped[:, d, 4 * i * P : 4 * (i + n) * P],
+                in_=y_grouped[i][0][:, d, :],
             )
 
         def qy(i, d):
@@ -316,7 +325,7 @@ def tile_feature_distillation_gradient_h1_kernel(
         def store_codes(i, n, part=slice(0, GD)):
             nc.sync.dma_start(
                 out=out_1.rearrange("g p m t -> p g (m t)")[:, part, 4 * i * P : 4 * (i + n) * P].bitcast(I32),
-                in_=y_codes[:, part, i * P : (i + n) * P].bitcast(I32),
+                in_=y_codes[i][:, part, :].bitcast(I32),
             )
 
         def store_plane(r, engine):
@@ -327,256 +336,249 @@ def tile_feature_distillation_gradient_h1_kernel(
 
         make_identity(nc, ident[:])
         load_x(0, cols(0))
-        txg(0, 0)
         load_x(0, cols(1))
+        load_lam()
+        zero_plane(p_plane, 0)
+        txg(0, 0)
         txg(0, 1)
         load_x(1)
-        load_lam()
-        tx(1)
-        zero_plane(p_plane, cols(0, 2 * K))
-        load_codes(p_codes, p_words, cols(0, 2 * K))
-        cxv(0, 0)
-        load_plane(p_plane, p_scales, cols(0, 2 * K), 0)
-        load_plane(p_plane, p_scales, cols(0, 2 * K), 1)
-        load_plane(p_plane, p_scales, cols(0, 2 * K), 2)
-        load_plane(p_plane, p_scales, cols(0, 2 * K), 3)
-        load_x(2)
-        load_codes(p_codes, p_words, cols(1, 2 * K))
-        zero_plane(p_plane, cols(1, 2 * K))
-        cxg(0, 1)
-        cx(1)
-        load_gamma()
-        tc_lam(0)
-        px(2)
+        cxg(0, 0)
         qxg(0, 0)
+        load_codes(p_codes, p_words, 0)
+        load_plane(p_plane, p_scales, 0, 0)
+        load_plane(p_plane, p_scales, 0, 1)
+        load_plane(p_plane, p_scales, 0, 2)
+        load_plane(p_plane, p_scales, 0, 3)
+        tx(1)
+        cxv(0, 1)
+        zero_plane(p_plane, 1)
         qxg(0, 1)
-        load_h(0, cols(0, 2 * K))
+        cx(1)
+        zero_plane(r_plane, 0)
+        zero_plane(r_plane, 1)
+        load_x(2)
+        px(2)
+        load_codes(p_codes, p_words, 2)
+        tc_lam(0)
         m1(0, 0)
-        load_h(1, cols(0, 2 * K))
-        load_plane(p_plane, p_scales, cols(1, 2 * K), 0)
-        load_plane(p_plane, p_scales, cols(1, 2 * K), 1)
-        load_plane(p_plane, p_scales, cols(1, 2 * K), 2)
-        load_plane(p_plane, p_scales, cols(1, 2 * K), 3)
-        zero_plane(r_plane, cols(0))
+        qx(1)
+        load_h(0, cols(0, 2 * K))
         cc_lam(0)
         tp(2)
-        load_codes(p_codes, p_words, cols(2, 2 * K))
-        qx(1)
-        load_codes(p_codes, p_words, cols(3, 2 * K))
-        cx(2)
-        sub(0, 0)
+        load_codes(p_codes, p_words, 1)
+        load_h(1, cols(0, 2 * K))
         m1(1, 0)
+        sub(0, 0)
+        vmul(0, 0)
+        sub(1, 0)
+        load_plane(p_plane, p_scales, 1, 0)
+        load_plane(p_plane, p_scales, 1, 1)
+        load_plane(p_plane, p_scales, 1, 2)
+        load_plane(p_plane, p_scales, 1, 3)
+        load_codes(p_codes, p_words, 3)
+        load_h(0, cols(1, 2 * K))
+        load_x(3)
+        cx(2)
         m1(0, 1)
-        zero_plane(r_plane, cols(1))
+        px(3)
+        sub(0, 1)
+        load_h(1, cols(1, 2 * K))
         m1(1, 1)
+        gmul(0, 1)
         m1(0, 2)
         m1(0, 3)
         m1(1, 2)
-        sub(1, 0)
-        sub(0, 1)
         qx(2)
-        load_h(0, cols(1, 2 * K))
-        gmul(0, 0)
-        load_x(3)
-        load_h(1, cols(1, 2 * K))
+        m1(1, 3)
+        m1(2, 0)
         load_x(4)
+        px(4)
+        tc_lam(1)
+        load_x(5)
         sub(1, 1)
         sub(0, 2)
-        load_h(2, cols(0, 2 * K))
-        gmul(0, 1)
-        m1(1, 3)
-        load_x(5)
-        tc_lam(1)
+        tp(3)
+        tp(4)
+        load_h(2, cols(1, 2 * K))
         gmul(1, 0)
         sub(0, 3)
-        tc_gamma()
-        px(3)
-        gmul(1, 1)
-        tp(3)
-        te(0, 0)
-        px(4)
-        cx(3)
-        sub(1, 2)
-        load_codes(r_codes, r_words, cols(0, 2 * K))
-        cc_lam(1)
-        m1(2, 0)
-        load_h(2, cols(1, 2 * K))
-        m1(2, 1)
-        vmulp(0, 2)
-        vmulp(0, 3)
-        sub(1, 3)
-        ce(0, 0)
-        m1(2, 2)
-        load_plane(r_plane, r_scales, cols(1), 0)
-        load_plane(r_plane, r_scales, cols(1), 1)
-        load_plane(r_plane, r_scales, cols(1), 2)
-        load_plane(r_plane, r_scales, cols(1), 3)
-        sub(2, 0)
-        m1(2, 3)
-        qx(3)
         px(5)
-        te(0, 1)
-        sub(2, 1)
-        cc_gamma()
-        tp(4)
-        sub(2, 2)
-        tp(5)
-        vmulp(1, 2)
-        vmulp(1, 3)
-        te(1, 0)
-        gmul(2, 0)
+        sub(1, 2)
+        gmul(1, 1)
+        cx(3)
+        sub(1, 3)
         cx(4)
-        m1(3, 0)
-        ce(0, 1)
+        te(0, 0)
+        vm2(0)
+        vm2(1)
+        load_h(2, cols(0, 2 * K))
+        tp(5)
+        m1(2, 1)
+        load_plane(r_plane, r_scales, 1, 0)
+        load_plane(r_plane, r_scales, 1, 1)
+        load_plane(r_plane, r_scales, 1, 2)
+        load_plane(r_plane, r_scales, 1, 3)
         cx(5)
-        sub(2, 3)
-        ce(1, 0)
-        m1(3, 1)
-        m1(3, 2)
-        qe2(0)
-        m1(3, 3)
-        gmul(2, 1)
-        te(1, 1)
-        ce(1, 1)
+        load_gamma()
+        m1(2, 2)
+        qx(3)
+        tc_gamma()
+        ce(0, 0)
         load_h(3)
-        te(2, 0)
-        sub(3, 0)
-        ce(2, 0)
+        te(0, 1)
+        load_plane(r_plane, r_scales, 0, 0)
+        load_plane(r_plane, r_scales, 0, 1)
+        load_plane(r_plane, r_scales, 0, 2)
+        load_plane(r_plane, r_scales, 0, 3)
+        sub(2, 0)
+        te(1, 0)
         qxr(4, 2)
-        vmulp(2, 2)
-        load_plane(r_plane, r_scales, cols(0), 0)
-        load_plane(r_plane, r_scales, cols(0), 1)
-        load_plane(r_plane, r_scales, cols(0), 2)
-        load_plane(r_plane, r_scales, cols(0), 3)
-        vmulp(2, 3)
-        m2(0, 0)
-        load_h(5)
-        gmul(3, 0)
+        te(1, 1)
+        load_codes(r_codes, r_words, 0)
+        ce(0, 1)
+        load_codes(r_codes, r_words, 1)
+        ce(1, 0)
+        gmul(2, 0)
+        m1(2, 3)
+        load_h(4)
+        sub(2, 1)
+        sub(2, 2)
+        m1(3, 0)
+        sub(2, 3)
+        m1(3, 1)
+        qe2(0)
+        m1(3, 2)
+        vmul(2, 1)
+        m1(3, 3)
+        ce(1, 1)
+        sub(3, 0)
         m1(4, 0)
-        sub(3, 1)
         qe2(1)
         m1(4, 1)
-        m1(4, 2)
-        load_codes(r_codes, r_words, cols(1, 2 * K))
+        cc_gamma()
+        sub(3, 1)
+        vm2(2)
         sub(3, 2)
-        load_h(4)
+        load_h(5)
         sub(3, 3)
+        gmul(3, 0)
+        m2(0, 0)
+        m2(0, 1)
         sub(4, 0)
+        gmul(3, 1)
         gam(0, 0)
         store_y(0, 0)
         sub(4, 1)
-        m2(0, 1)
-        m1(4, 3)
         m2(1, 0)
-        gam(0, 1)
-        store_y(0, 1)
+        vm2(3)
+        te(2, 0)
         te(2, 1)
-        sub(4, 2)
-        gam(1, 0)
-        store_y(1, 0)
-        gmul(3, 1)
-        vmulp(3, 2)
-        cast(0, 0)
-        gmul(3, 3)
-        ce(2, 1)
+        ce(2, 0)
         te(3, 0)
-        m2(1, 1)
+        m1(4, 2)
+        m1(4, 3)
+        ce(2, 1)
+        sub(4, 2)
         m1(5, 0)
-        cast(0, 1)
-        m1(5, 1)
         sub(4, 3)
-        gmul(4, 0)
+        m1(5, 1)
+        m1(5, 2)
         ce(3, 0)
-        te(3, 1)
+        gmul(4, 0)
         gmul(4, 1)
         sub(5, 0)
         qe2(2)
-        ty(0, (0, 1))
-        cast(1, 0)
-        cy(0, (0, 1))
+        m2(1, 1)
+        te(3, 1)
+        gam(0, 1)
+        store_y(0, 1)
+        ce(3, 1)
+        te(4, 0)
+        ce(4, 0)
+        sub(5, 1)
+        cast(0, 0)
+        gam(1, 0)
+        store_y(1, 0)
+        m2(2, 0)
+        m1(5, 3)
         gam(1, 1)
         store_y(1, 1)
-        te(4, 0)
-        ce(3, 1)
-        sub(5, 1)
-        m1(5, 2)
-        vmulp(4, 2)
-        vmulp(4, 3)
-        gmul(5, 0)
-        sub(5, 2)
-        cast(1, 1)
-        m1(5, 3)
-        qe2(3)
-        m2(2, 0)
         m2(2, 1)
-        ce(4, 0)
-        gmul(5, 1)
+        cast(0, 1)
+        vm2(4)
+        cast(1, 0)
+        gmul(5, 0)
         te(4, 1)
-        gam(2, 0)
-        store_y(2, 0)
-        ty(1, (0, 1))
+        gmul(5, 1)
+        qe2(3)
+        sub(5, 2)
         sub(5, 3)
-        gam(2, 1)
-        store_y(2, 1)
-        ce(4, 1)
-        cast(2, 0)
+        ty(0, (0, 1))
         te(5, 0)
-        ce(5, 0)
+        ce(4, 1)
         m2(3, 0)
         m2(3, 1)
-        gmul(5, 2)
-        cast(2, 1)
-        vmulp(5, 3)
+        cy(0, (0, 1))
+        gam(2, 0)
+        store_y(2, 0)
+        vm2(5)
+        te(5, 1)
         qe2(4)
+        cast(1, 1)
+        cast(2, 0)
+        gam(2, 1)
+        store_y(2, 1)
+        ty(1, (0, 1))
+        m2(4, 0)
         gam(3, 0)
         store_y(3, 0)
-        cy(1, (0, 1))
+        ce(5, 0)
+        ce(5, 1)
         gam(3, 1)
         store_y(3, 1)
-        te(5, 1)
-        ty(2, (0, 1))
         qe(5, 0)
-        ce(5, 1)
-        cast(3, 0)
-        m2(4, 0)
-        cast(3, 1)
-        gam(4, 0)
-        store_y(4, 0)
-        cy(2, (0, 1))
+        cast(2, 1)
         qe(5, 1)
         m2(4, 1)
-        ty(3, (0, 1))
+        gam(4, 0)
+        store_y(4, 0)
+        cast(3, 0)
+        cast(3, 1)
+        ty(2, (0, 1))
         gam(4, 1)
         store_y(4, 1)
-        cast(4, 0)
+        cy(1, (0, 1))
+        ty(3, (0, 1))
+        cy(2, (0, 1))
         m2(5, 0)
         qyr(0, 0, 2)
         qyr(1, 0, 2)
         store_codes(0, 2)
-        cy(3, (0, 1))
         gam(5, 0)
         store_y(5, 0)
-        m2(5, 1)
+        cy(3, (0, 1))
+        cast(4, 0)
         qyr(0, 2, 2)
         qyr(1, 2, 2)
         store_codes(2, 2)
         cast(4, 1)
         cast(5, 0)
-        ty(4, (0, 1))
-        ty(5, (0,))
-        cy(4, (0, 1))
+        m2(5, 1)
         gamb(5, 1)
+        ty(4, (0, 1))
         gam(5, 1)
         store_y(5, 1)
-        cy(5, (0,))
+        ty(5, (0,))
+        cy(4, (0, 1))
+        ty(5, (1,))
         qyr(0, 4, 1)
         qyr(1, 4, 1)
         store_codes(4, 1)
-        ty(5, (1,))
-        cyv(5, (1,))
+        cy(5, (0,))
+        cy(5, (1,))
         qy(5, 0)
-        qy(5, 1)
         store_codes(5, 1, slice(0, 1))
+        qy(5, 1)
         store_codes(5, 1, slice(1, 2))
         store_plane(0, nc.sync)
         store_plane(1, nc.scalar)

from contextlib import ExitStack

import concourse.mybir as mybir
from concourse.masks import make_identity

M, D, F = 768, 1024, 2048
FLOPS = 2 * 2 * M * D * F

F32 = mybir.dt.float32
BF16 = mybir.dt.bfloat16
I32 = mybir.dt.int32
U32 = mybir.dt.uint32
U8 = mybir.dt.uint8
FP8X4 = mybir.dt.float8_e4m3fn_x4
FP4X4 = mybir.dt.float4_e2m1fn_x4
SUB = mybir.AluOpType.subtract
MULT = mybir.AluOpType.mult

P = 128
K = 512
TILES = M // P
GD = D // K
GF = F // K
Y_GROUPS = ((0, 2), (2, 2), (4, 1), (5, 1))


def tile_feature_distillation_gradient_h1_kernel(
    tc, x, p_words, p_scales, h, lam, r_words, r_scales, gamma, out_0, out_1, out_2
):
    nc = tc.nc
    with ExitStack() as ctx:
        keep = ctx.enter_context(tc.tile_pool(name="keep", bufs=1))
        work = ctx.enter_context(tc.tile_pool(name="work", bufs=4))
        psum = ctx.enter_context(tc.psum_pool(name="psum", bufs=1))
        ctx.enter_context(tc.manual_schedule())

        def kept(name, shape, dtype):
            return keep.tile(shape, dtype, name=name, align_bytes=64)

        ident = kept("ident", [P, P], F32)
        x_sb = [kept("x%d" % i, [P, D], BF16) for i in range(TILES)]
        h_sb = [kept("h%d" % i, [P, F], BF16) for i in range(TILES)]
        p_codes = [kept("p_codes%d" % c, [P, GD, 2 * K], U8) for c in range(GF)]
        p_plane = [kept("p_plane%d" % a, [P, GD, 2 * K], U8) for a in range(2)]
        r_codes = [kept("r_codes%d" % d, [P, GF, 2 * K], U8) for d in range(GD)]
        r_plane = [kept("r_plane%d" % d, [P, GF, K], U8) for d in range(GD)]
        lam_rows = kept("lam_rows", [P, GF, 4], BF16)
        gamma_rows = kept("gamma_rows", [P, 8], BF16)
        lam_all = kept("lam_all", [P, F], BF16)
        gamma_all = kept("gamma_all", [P, D], BF16)
        x_grouped = kept("x_grouped", [P, TILES * D], BF16)
        x_codes = kept("x_codes", [P, TILES * GD * P], U32)
        x_plane = kept("x_plane", [P, TILES * GD * P], U8)
        e_codes = [kept("e_codes%d" % i, [P, GF * P], U32) for i in range(TILES)]
        e_plane = [kept("e_plane%d" % i, [P, GF * P], U8) for i in range(TILES)]
        e_bf = [kept("e_bf%d" % i, [P, F], BF16) for i in range(TILES)]
        y_f32 = [kept("y_f32_%d" % i, [P, D], F32) for i in range(TILES)]
        y_bf = [kept("y_bf%d" % i, [P, D], BF16) for i in range(TILES)]
        y_grouped = {}
        y_codes = {}
        for first, count in Y_GROUPS:
            grouped = kept("y_grouped%d" % first, [P, GD, 4 * P * count], BF16)
            codes = kept("y_codes%d" % first, [P, GD, P * count], U32)
            for j in range(count):
                y_grouped[first + j] = (grouped, j)
            y_codes[first] = codes
        y_plane = kept("y_plane", [P, GD, M], U8)

        lam_bank = psum.tile([P, K], F32, name="lam_bank")
        e_grouped = [kept("e_grouped%d" % i, [P, F], BF16) for i in range(TILES)]
        free_banks = list(range(7))
        bank_of = {}

        def take_bank(key):
            k = free_banks[0]
            free_banks.remove(k)
            bank_of[key] = k
            held[key] = psum.tile([P, K], F32, name="bank%d" % k)
            return held[key]

        def give_bank(key):
            free_banks.append(bank_of[key])
            return held[key]

        held = {}
        diffs = {}

        def rows(i):
            return slice(i * P, (i + 1) * P)

        def cols(c, width=K):
            return slice(c * width, (c + 1) * width)

        def by_word_half(ap):
            return ap.rearrange("m (p u e) -> m u p e", u=2, e=2)

        def as_word_half(ap):
            return ap.rearrange("m (u p e) -> m u p e", u=2, e=2)

        def zero_plane(planes, a):
            nc.vector.memset(planes[a][:].rearrange("p g n -> p (g n)").bitcast(I32), 0)

        def load_plane(planes, scales, a, r):
            width = planes[a].shape[2]
            nc.sync.dma_start(
                out=planes[a][r:P:32, :, :].bitcast(I32),
                in_=scales[:, r:16:4, cols(a, width)].rearrange("g q n -> q g n").bitcast(I32),
            )

        def load_codes(codes, words, c):
            nc.sync.dma_start(
                out=codes[c][:].bitcast(I32),
                in_=words[:, :, cols(c, 2 * K)].rearrange("g p n -> p g n").bitcast(I32),
            )

        def load_x(i, part=slice(0, D)):
            nc.sync.dma_start(out=x_sb[i][:, part], in_=x[rows(i), part])

        def load_h(i, part=slice(0, F)):
            nc.sync.dma_start(out=h_sb[i][:, part], in_=h[rows(i), part])

        def load_lam():
            nc.scalar.dma_start(out=lam_rows[:], in_=lam.rearrange("(c p t) -> p c t", p=P, t=4))

        def load_gamma():
            nc.sync.dma_start(out=gamma_rows[:], in_=gamma.rearrange("(p t) -> p t", p=P))

        def turn(key, sources, bank=None):
            if bank is None:
                bank = take_bank(key)
            for j, source in enumerate(sources):
                nc.tensor.transpose(bank[:, cols(j, P)], source, ident[:])
            held[key] = bank

        def gather(key, groups, target, copy):
            bank = give_bank(key)
            copy(
                out=target.bitcast(F32).rearrange("p g (m u) -> p g m u", u=2),
                in_=bank[:, : groups * 2 * P].rearrange("p (g u m) -> p g m u", g=groups, u=2),
            )

        def tc_lam(half):
            words = lam_rows[:].rearrange("p c t -> p (c t)").bitcast(F32)
            turn(("lam", half), [words[:, j : j + 1].to_broadcast([P, P]) for j in range(4 * half, 4 * half + 4)], lam_bank if half == 1 else None)

        def cc_lam(half):
            nc.scalar.copy(out=lam_all[:, cols(half, 2 * K)].bitcast(F32), in_=(lam_bank if half == 1 else give_bank(("lam", half)))[:])

        def tc_gamma():
            words = gamma_rows[:].bitcast(F32)
            turn(("gamma",), [words[:, j : j + 1].to_broadcast([P, P]) for j in range(4)])

        def cc_gamma():
            nc.scalar.copy(
                out=gamma_all[:].bitcast(F32).rearrange("q (p j) -> q p j", j=4),
                in_=give_bank(("gamma",))[:].rearrange("q (j p) -> q p j", j=4),
            )

        def tx(i):
            words = x_sb[i][:].bitcast(F32)
            turn(("x", i), [words[:, 256 * g + u : 256 * (g + 1) : 2] for g in range(GD) for u in range(2)])

        def txg(i, g):
            words = x_sb[i][:].bitcast(F32)
            turn(("x", i, g), [words[:, 256 * g + u : 256 * (g + 1) : 2] for u in range(2)])

        def x_target(first, count):
            return x_grouped[:, first * K : (first + count) * K].rearrange("p (g n) -> p g n", g=count)

        def cxg(i, g):
            gather(("x", i, g), 1, x_target(GD * i + g, 1), nc.scalar.copy)

        def cxv(i, g):
            gather(("x", i, g), 1, x_target(GD * i + g, 1), nc.vector.tensor_copy)

        def quantize_x(first, count):
            nc.vector.quantize_mx(
                out=x_codes[:, first * P : (first + count) * P].bitcast(FP8X4),
                scales=x_plane[:, first * P : (first + count) * P],
                in_=x_grouped[:, first * K : (first + count) * K],
            )

        def qxg(i, g):
            quantize_x(GD * i + g, 1)

        def cx(i):
            gather(("x", i), GD, x_target(GD * i, GD), nc.scalar.copy)

        def qx(i):
            quantize_x(GD * i, GD)

        def qxr(i, n):
            quantize_x(GD * i, GD * n)

        def m1(i, c):
            bank = take_bank(("s1", i, c))
            for g in range(GD):
                nc.tensor.matmul_mx(
                    out=bank[:],
                    lhsT=x_codes[:, cols(GD * i + g, P)].bitcast(FP8X4),
                    lhsT_scale=x_plane[:, cols(GD * i + g, P)],
                    rhs=p_codes[c][:, g, :].bitcast(FP4X4),
                    rhs_scale=p_plane[c // 2][:, g, cols(c % 2)],
                    start=(g == 0),
                    stop=(g == GD - 1),
                )

        def sub(i, c):
            if (i, c // 2) not in diffs:
                diffs[(i, c // 2)] = work.tile([P, 2 * K], F32, name="diff", align_bytes=64, bufs=5)
            diff = diffs[(i, c // 2)][:, cols(c % 2)]
            bank = give_bank(("s1", i, c))
            nc.vector.tensor_tensor(
                out=as_word_half(diff), in0=by_word_half(bank[:]), in1=by_word_half(h_sb[i][:, cols(c)]), op=SUB
            )
            held[("diff", i, c)] = diff

        def mul(engine, i, c):
            engine.tensor_tensor(
                out=e_bf[i][:, cols(c)], in0=held.pop(("diff", i, c)), in1=lam_all[:, cols(c)], op=MULT
            )

        def gmul(i, c):
            mul(nc.gpsimd, i, c)

        def vmul(i, c):
            mul(nc.vector, i, c)

        def vmulp(i, c):
            nc.vector.tensor_tensor(
                out=e_bf[i][:, cols(c)],
                in0=held.pop(("diff", i, c)),
                in1=lam_bank[:].bitcast(BF16)[:, cols(c - 2)],
                op=MULT,
            )

        def vm2(i):
            nc.vector.tensor_tensor(
                out=e_bf[i][:, cols(1, 2 * K)], in0=diffs[(i, 1)][:], in1=lam_bank[:].bitcast(BF16), op=MULT
            )

        def te(i, half):
            words = e_bf[i][:].bitcast(F32)
            turn(("e", i, half), [words[:, cols(j, P)] for j in range(4 * half, 4 * half + 4)])

        def ce(i, half):
            target = e_grouped[i][:, cols(half, 2 * K)].rearrange("p (g n) -> p g n", g=2)
            gather(("e", i, half), 2, target, nc.scalar.copy)

        def qe(i, half):
            nc.vector.quantize_mx(
                out=e_codes[i][:, cols(half, 2 * P)].bitcast(FP8X4),
                scales=e_plane[i][:, cols(half, 2 * P)],
                in_=e_grouped[i][:, cols(half, 2 * K)],
            )

        def qe2(i):
            nc.vector.quantize_mx(out=e_codes[i][:].bitcast(FP8X4), scales=e_plane[i][:], in_=e_grouped[i][:])

        def px(i):
            words = work.tile([P, K], F32, name="x_words", bufs=4)
            nc.scalar.copy(
                out=words[:].rearrange("m (g u p) -> m g u p", g=GD, u=2),
                in_=x_sb[i][:].bitcast(F32).rearrange("m (g p u) -> m g u p", g=GD, u=2),
            )
            held[("x_words", i)] = words

        def tp(i):
            words = held.pop(("x_words", i))
            turn(("x", i), [words[:, cols(j, P)] for j in range(4)])

        def m2(i, d):
            bank = take_bank(("s2", i, d))
            for g in range(GF):
                nc.tensor.matmul_mx(
                    out=bank[:],
                    lhsT=e_codes[i][:, cols(g, P)].bitcast(FP8X4),
                    lhsT_scale=e_plane[i][:, cols(g, P)],
                    rhs=r_codes[d][:, g, :].bitcast(FP4X4),
                    rhs_scale=r_plane[d][:, g, :],
                    start=(g == 0),
                    stop=(g == GF - 1),
                )

        def gam(i, d):
            nc.vector.tensor_tensor(
                out=y_f32[i][:, cols(d)], in0=give_bank(("s2", i, d))[:], in1=gamma_all[:, cols(d)], op=MULT
            )

        def gamb(i, d):
            nc.vector.tensor_tensor(
                out=as_word_half(y_bf[i][:, cols(d)]),
                in0=by_word_half(held[("s2", i, d)][:]),
                in1=by_word_half(gamma_all[:, cols(d)]),
                op=MULT,
            )

        def cast(i, d):
            nc.scalar.copy(out=as_word_half(y_bf[i][:, cols(d)]), in_=by_word_half(y_f32[i][:, cols(d)]))

        def store_y(i, d):
            nc.sync.dma_start(out=out_0[rows(i), cols(d)], in_=y_f32[i][:, cols(d)])

        def ty(i, ds):
            words = y_bf[i][:].bitcast(F32)
            turn(("y", i, ds), [words[:, cols(2 * d + u, P)] for d in ds for u in range(2)])

        def cyv(i, ds):
            cy(i, ds, nc.vector.tensor_copy)

        def cy(i, ds, copy=nc.scalar.copy):
            grouped, j = y_grouped[i]
            gather(("y", i, ds), len(ds), grouped[:, ds[0] : ds[-1] + 1, cols(j, 4 * P)], copy)

        def qyr(d, i, n):
            nc.vector.quantize_mx(
                out=y_codes[i][:, d, :].bitcast(FP8X4),
                scales=y_plane[:, d, i * P : (i + n) * P],
                in_=y_grouped[i][0][:, d, :],
            )

        def qy(i, d):
            qyr(d, i, 1)

        def store_codes(i, n, part=slice(0, GD)):
            nc.sync.dma_start(
                out=out_1.rearrange("g p m t -> p g (m t)")[:, part, 4 * i * P : 4 * (i + n) * P].bitcast(I32),
                in_=y_codes[i][:, part, :].bitcast(I32),
            )

        def store_plane(r, engine):
            engine.dma_start(
                out=out_2[:, r:16:4, :].rearrange("g q m -> q g m").bitcast(I32),
                in_=y_plane[r:P:32, :, :].bitcast(I32),
            )

        make_identity(nc, ident[:])
        load_x(0, cols(0))
        load_x(0, cols(1))
        load_lam()
        zero_plane(p_plane, 0)
        txg(0, 0)
        txg(0, 1)
        load_x(1)
        cxg(0, 0)
        qxg(0, 0)
        load_codes(p_codes, p_words, 0)
        load_plane(p_plane, p_scales, 0, 0)
        load_plane(p_plane, p_scales, 0, 1)
        load_plane(p_plane, p_scales, 0, 2)
        load_plane(p_plane, p_scales, 0, 3)
        tx(1)
        cxv(0, 1)
        zero_plane(p_plane, 1)
        qxg(0, 1)
        cx(1)
        zero_plane(r_plane, 0)
        zero_plane(r_plane, 1)
        load_x(2)
        px(2)
        load_codes(p_codes, p_words, 2)
        tc_lam(0)
        m1(0, 0)
        qx(1)
        load_h(0, cols(0, 2 * K))
        cc_lam(0)
        tp(2)
        load_codes(p_codes, p_words, 1)
        load_h(1, cols(0, 2 * K))
        m1(1, 0)
        sub(0, 0)
        vmul(0, 0)
        sub(1, 0)
        load_plane(p_plane, p_scales, 1, 0)
        load_plane(p_plane, p_scales, 1, 1)
        load_plane(p_plane, p_scales, 1, 2)
        load_plane(p_plane, p_scales, 1, 3)
        load_codes(p_codes, p_words, 3)
        load_h(0, cols(1, 2 * K))
        load_x(3)
        cx(2)
        m1(0, 1)
        px(3)
        sub(0, 1)
        load_h(1, cols(1, 2 * K))
        m1(1, 1)
        gmul(0, 1)
        m1(0, 2)
        m1(0, 3)
        m1(1, 2)
        qx(2)
        m1(1, 3)
        m1(2, 0)
        load_x(4)
        px(4)
        tc_lam(1)
        load_x(5)
        sub(1, 1)
        sub(0, 2)
        tp(3)
        tp(4)
        load_h(2, cols(1, 2 * K))
        gmul(1, 0)
        sub(0, 3)
        px(5)
        sub(1, 2)
        gmul(1, 1)
        cx(3)
        sub(1, 3)
        cx(4)
        te(0, 0)
        vm2(0)
        vm2(1)
        load_h(2, cols(0, 2 * K))
        tp(5)
        m1(2, 1)
        load_plane(r_plane, r_scales, 1, 0)
        load_plane(r_plane, r_scales, 1, 1)
        load_plane(r_plane, r_scales, 1, 2)
        load_plane(r_plane, r_scales, 1, 3)
        cx(5)
        load_gamma()
        m1(2, 2)
        qx(3)
        tc_gamma()
        ce(0, 0)
        load_h(3)
        te(0, 1)
        load_plane(r_plane, r_scales, 0, 0)
        load_plane(r_plane, r_scales, 0, 1)
        load_plane(r_plane, r_scales, 0, 2)
        load_plane(r_plane, r_scales, 0, 3)
        sub(2, 0)
        te(1, 0)
        qxr(4, 2)
        te(1, 1)
        load_codes(r_codes, r_words, 0)
        ce(0, 1)
        load_codes(r_codes, r_words, 1)
        ce(1, 0)
        gmul(2, 0)
        m1(2, 3)
        load_h(4)
        sub(2, 1)
        sub(2, 2)
        m1(3, 0)
        sub(2, 3)
        m1(3, 1)
        qe2(0)
        m1(3, 2)
        vmul(2, 1)
        m1(3, 3)
        ce(1, 1)
        sub(3, 0)
        m1(4, 0)
        qe2(1)
        m1(4, 1)
        cc_gamma()
        sub(3, 1)
        vm2(2)
        sub(3, 2)
        load_h(5)
        sub(3, 3)
        gmul(3, 0)
        m2(0, 0)
        m2(0, 1)
        sub(4, 0)
        gmul(3, 1)
        gam(0, 0)
        store_y(0, 0)
        sub(4, 1)
        m2(1, 0)
        vm2(3)
        te(2, 0)
        te(2, 1)
        ce(2, 0)
        te(3, 0)
        m1(4, 2)
        m1(4, 3)
        ce(2, 1)
        sub(4, 2)
        m1(5, 0)
        sub(4, 3)
        m1(5, 1)
        m1(5, 2)
        ce(3, 0)
        gmul(4, 0)
        gmul(4, 1)
        sub(5, 0)
        qe2(2)
        m2(1, 1)
        te(3, 1)
        gam(0, 1)
        store_y(0, 1)
        ce(3, 1)
        te(4, 0)
        ce(4, 0)
        sub(5, 1)
        cast(0, 0)
        gam(1, 0)
        store_y(1, 0)
        m2(2, 0)
        m1(5, 3)
        gam(1, 1)
        store_y(1, 1)
        m2(2, 1)
        cast(0, 1)
        vm2(4)
        cast(1, 0)
        gmul(5, 0)
        te(4, 1)
        gmul(5, 1)
        qe2(3)
        sub(5, 2)
        sub(5, 3)
        ty(0, (0, 1))
        te(5, 0)
        ce(4, 1)
        m2(3, 0)
        m2(3, 1)
        cy(0, (0, 1))
        gam(2, 0)
        store_y(2, 0)
        vm2(5)
        te(5, 1)
        qe2(4)
        cast(1, 1)
        cast(2, 0)
        gam(2, 1)
        store_y(2, 1)
        ty(1, (0, 1))
        m2(4, 0)
        gam(3, 0)
        store_y(3, 0)
        ce(5, 0)
        ce(5, 1)
        gam(3, 1)
        store_y(3, 1)
        qe(5, 0)
        cast(2, 1)
        qe(5, 1)
        m2(4, 1)
        gam(4, 0)
        store_y(4, 0)
        cast(3, 0)
        cast(3, 1)
        ty(2, (0, 1))
        gam(4, 1)
        store_y(4, 1)
        cy(1, (0, 1))
        ty(3, (0, 1))
        cy(2, (0, 1))
        m2(5, 0)
        qyr(0, 0, 2)
        qyr(1, 0, 2)
        store_codes(0, 2)
        gam(5, 0)
        store_y(5, 0)
        cy(3, (0, 1))
        cast(4, 0)
        qyr(0, 2, 2)
        qyr(1, 2, 2)
        store_codes(2, 2)
        cast(4, 1)
        cast(5, 0)
        m2(5, 1)
        gamb(5, 1)
        ty(4, (0, 1))
        gam(5, 1)
        store_y(5, 1)
        ty(5, (0,))
        cy(4, (0, 1))
        ty(5, (1,))
        qyr(0, 4, 1)
        qyr(1, 4, 1)
        store_codes(4, 1)
        cy(5, (0,))
        cy(5, (1,))
        qy(5, 0)
        store_codes(5, 1, slice(0, 1))
        qy(5, 1)
        store_codes(5, 1, slice(1, 2))
        store_plane(0, nc.sync)
        store_plane(1, nc.scalar)
        store_plane(2, nc.sync)
        store_plane(3, nc.scalar)
